import numpy as np
import ml_dtypes


def mxq(x, axis, fmt="e4m3"):
    dtype, down = {"e4m3": (ml_dtypes.float8_e4m3fn, 7), "e5m2": (ml_dtypes.float8_e5m2, 14)}[fmt]
    v = np.moveaxis(np.asarray(x, np.float32).astype(ml_dtypes.bfloat16).astype(np.float64), axis, -1)
    blocks = v.reshape(v.shape[:-1] + (-1, 32))
    amax = np.abs(blocks).max(-1, keepdims=True)
    byte = np.maximum(np.where(amax > 0, np.frexp(amax)[1] - 1 + 127, 0) - down, 1)
    scale = np.exp2(byte - 127.0)
    codes = (blocks / scale).astype(np.float32).astype(dtype).astype(np.float64)
    return np.moveaxis((codes * scale).reshape(v.shape), -1, axis)


WIDE = False


def mx_kscale(k):
    if not WIDE:
        return np.ones(k)
    levels = np.array([10, -10, 5, -5, 0])
    if k % 512:
        return np.exp2(np.random.permutation(np.resize(levels, k // 32))).repeat(32)
    a = np.empty((k // 512, 16))
    for p in range(k // 512):
        a[p, :8] = np.random.permutation(np.resize(levels, 8))
        for g in range(8):
            far = levels[np.abs(levels - a[p, g]) >= 10]
            a[p, g + 8] = far[np.random.randint(len(far))]
    return np.exp2(a.ravel()).repeat(32)


def f64(x):
    return np.asarray(x).astype(np.float64)


def striped(idx):
    return np.tile(idx.reshape(-1, 16).T, (8, 1)).astype(np.uint16)


def unstriped(offs):
    return offs[:16].T.reshape(-1).astype(np.int64)


def striped8(idx):
    return np.concatenate([x.reshape(-1, 16).T for x in idx]).astype(np.uint16)


def runs(offs, k):
    lists = np.stack([offs[16 * r : 16 * r + 16].T.reshape(-1) for r in range(8)]).astype(np.int64)
    return lists[np.arange(k) % 512 // 64]


def pack_weight(w):
    k, n = w.shape
    w = f64(np.asarray(w, np.float32).astype(ml_dtypes.bfloat16)).reshape(k // 32, 32, n)
    amax = np.abs(w).max(1)
    byte = np.clip(np.where(amax > 0, np.frexp(amax)[1] - 1 + 127 - 7, 1), 1, 254)
    scaled = (w * np.exp2(127.0 - byte)[:, None, :]).reshape(k, n).astype(np.float32)
    words = np.ascontiguousarray(scaled.reshape(k // 512, 128, 4, n).transpose(0, 1, 3, 2)).astype(ml_dtypes.float8_e4m3fn).view(np.uint8)
    return words, np.ascontiguousarray(byte.astype(np.uint8).reshape(k // 512, 16, n))


def unpack_weight(words, scales):
    g, p, n, _ = words.shape
    vals = np.ascontiguousarray(words).view(ml_dtypes.float8_e4m3fn).astype(np.float64) * np.repeat(np.exp2(scales.astype(np.float64) - 127.0), 8, axis=1)[..., None]
    return vals.transpose(0, 1, 3, 2).reshape(g * 512, n)


E2M1 = np.array([0.0, 0.5, 1.0, 1.5, 2.0, 3.0, 4.0, 6.0, -0.0, -0.5, -1.0, -1.5, -2.0, -3.0, -4.0, -6.0])


def pack_fp4(w):
    k, n = w.shape
    w = f64(np.asarray(w, np.float32).astype(ml_dtypes.bfloat16)).reshape(k // 32, 32, n)
    amax = np.abs(w).max(1)
    mant, ex = np.frexp(amax / 6.0)
    byte = np.clip(np.where(amax > 0, np.where(mant > 0.5, ex, ex - 1) + 127, 1), 1, 254)
    scaled = (w * np.exp2(127.0 - byte)[:, None, :]).reshape(k, n).astype(np.float32)
    c = np.ascontiguousarray(scaled.reshape(k // 512, 128, 4, n).transpose(0, 1, 3, 2)).astype(ml_dtypes.float4_e2m1fn).view(np.uint8) & 0xF
    words = (c[..., 0::2] | (c[..., 1::2] << 4)).reshape(k // 512, 128, 2 * n)
    return np.ascontiguousarray(words), np.ascontiguousarray(byte.astype(np.uint8).reshape(k // 512, 16, n))


def unpack_fp4(words, scales):
    g, _, n = scales.shape
    words = np.ascontiguousarray(words).reshape(g, 128, n, 2)
    nib = np.empty((g, 128, n, 4), np.uint8)
    nib[..., 0::2] = words & 0xF
    nib[..., 1::2] = words >> 4
    vals = E2M1[nib] * np.repeat(np.exp2(scales.astype(np.float64) - 127.0), 8, axis=1)[..., None]
    return vals.transpose(0, 1, 3, 2).reshape(g * 512, n)


def sigmoid(v):
    return 1.0 / (1.0 + np.exp(-np.maximum(v, -700.0)))

def planes(y):
    n, m = y.shape
    v = y.astype(np.float32).astype(ml_dtypes.bfloat16).astype(np.float64).reshape(n // 32, 32, m)
    top = np.abs(v).max(1)
    byte = np.clip(np.where(top > 0, np.frexp(top)[1] - 1 + 127 - 7, 1), 1, 254)
    codes = (v * np.exp2(127.0 - byte)[:, None, :]).reshape(n, m).astype(np.float32).astype(ml_dtypes.float8_e4m3fn).view(np.uint8)
    words = codes.reshape(n // 512, 128, 4, m).transpose(0, 1, 3, 2)
    return np.ascontiguousarray(words), np.ascontiguousarray(byte.astype(np.uint8).reshape(n // 512, 16, m))


K, T, S, V, H, W = 512, 2048, 512, 512, 512, 2048


def setup_inputs():
    n = np.random.standard_normal
    s = mx_kscale(K)[:, None]
    u = mx_kscale(S)
    packed_xT = pack_weight(n((K, T)) * s)
    packed_w1 = pack_fp4(n((K, H)) / np.sqrt(K) / s)
    packed_w2 = pack_fp4(n((K, H)) / np.sqrt(K) / s)
    packed_w3 = pack_fp4(n((K, H)) / np.sqrt(K) / s)
    return {
        "x_words": packed_xT[0],
        "x_scales": packed_xT[1],
        "w1_words": packed_w1[0],
        "w1_scales": packed_w1[1],
        "w2_words": packed_w2[0],
        "w2_scales": packed_w2[1],
        "w3_words": packed_w3[0],
        "w3_scales": packed_w3[1],
        "ga": (np.random.uniform(0.5, 1.5, (H, 1)) * u[:, None]).astype(np.float32),
        "gb": (np.random.uniform(0.5, 1.5, (H, 1)) / u[:, None]).astype(np.float32),
        "sl": np.random.uniform(1.0, 2.0, (S, 1)).astype(np.float32),
        "th": (0.5 * n((S, 1))).astype(np.float32),
        "sl2": np.random.uniform(1.0, 2.0, (S, 1)).astype(np.float32),
        "th2": (0.5 * n((S, 1))).astype(np.float32),
        "offs": striped(np.random.permutation(T)[:S]),
        "two": striped(np.random.permutation(T)[:S]),
        "n1": striped8(np.stack([np.random.permutation(S) for _ in range(8)])),
        "n2": striped8(np.stack([np.random.permutation(S) for _ in range(8)])),
        "n3": striped8(np.stack([np.random.permutation(S) for _ in range(8)])),
        "three": striped(np.random.permutation(T)[:V]),
        "n4": striped(np.random.randint(0, V, W)),
        "n5": striped(np.random.permutation(V)),
        "n6": striped(np.random.permutation(V)),
    }


def reference(x_words, x_scales, w1_words, w1_scales, w2_words, w2_scales, w3_words, w3_scales, ga, gb, sl, th, sl2, th2, offs, two, n1, n2, n3, three, n4, n5, n6):
    xq = unpack_weight(x_words, x_scales)[:, unstriped(offs)]
    y = unpack_fp4(w1_words, w1_scales).T @ xq
    x_two = unpack_weight(x_words, x_scales)[:, unstriped(two)]
    d = unpack_fp4(w2_words, w2_scales).T @ x_two
    z = f64(ga) * (np.maximum(np.minimum(y - (0.5 * (y[np.arange(H)[:, None], runs(n1, H)])), d[np.arange(H)[:, None], runs(n2, H)]), d[np.arange(H)[:, None], runs(n3, H)]))
    x_three = unpack_weight(x_words, x_scales)[:, unstriped(three)]
    b = unpack_fp4(w3_words, w3_scales).T @ x_three
    mb = b[:, unstriped(n4)]
    mx = mb.reshape(H, V, 4).max(axis=2)
    mn = mb.reshape(H, V, 4).min(axis=2)
    z2 = f64(gb) * (np.maximum(np.minimum(1.5 * b, mx), mn))
    s = 0.0625 * ((mxq(z, 0, "e4m3").T @ mxq(z2, 0, "e4m3")))
    sg = sigmoid(f64(sl) * (s[:, unstriped(n5)] - f64(th)))
    sg2 = sigmoid(f64(sl2) * (f64(th2) - s[:, unstriped(n6)]))
    out_0 = 2.0 * ((s * sg) * sg2)
    return (out_0,) + planes(out_0)

@@ -1,0 +1,280 @@
+from contextlib import ExitStack
+
+import concourse.mybir as mybir
+
+FLOPS = 4 * 2 * 512 * 512 * 512
+
+F32 = mybir.dt.float32
+BF16 = mybir.dt.bfloat16
+I32 = mybir.dt.int32
+U32 = mybir.dt.uint32
+U16 = mybir.dt.uint16
+U8 = mybir.dt.uint8
+FP8X4 = mybir.dt.float8_e4m3fn_x4
+FP4X4 = mybir.dt.float4_e2m1fn_x4
+ALU = mybir.AluOpType
+ACT = mybir.ActivationFunctionType
+
+P = 128
+PACK = 4
+N = 512
+TOKENS = 2048
+PIECE = 256
+Z_PIECES = ((0, 256), (256, 384), (384, 512))
+OUT_PIECES = ((0, 256), (256, 384), (384, 512))
+MEMBER_PIECES_ON_VECTOR = 2
+
+
+def tile_picked_twkclampbgclipecr_none_po_kernel(
+    tc, x_words, x_scales, w1_words, w1_scales, w2_words, w2_scales, w3_words, w3_scales,
+    ga, gb, sl, th, sl2, th2, offs, two, n1, n2, n3, three, n4, n5, n6, out_0, out_1, out_2,
+):
+    nc = tc.nc
+    with ExitStack() as ctx:
+        keep = ctx.enter_context(tc.tile_pool(name="keep", bufs=1))
+        psum = ctx.enter_context(tc.psum_pool(name="psum", bufs=8))
+
+        def sb(name, shape, dtype):
+            return keep.tile(shape, dtype, name=name, align_bytes=64)
+
+        def load_list(name, src):
+            lst = keep.tile(list(src.shape), U16, name=name)
+            nc.sync.dma_start(lst[:], src)
+            return lst
+
+        def load_column(name, src, queue):
+            col = sb(name, [P, PACK], F32)
+            queue.dma_start(col[:], src.rearrange("(p t) o -> p (t o)", t=PACK))
+            return col
+
+        def load_scale_rows(dst, src):
+            for q in range(4):
+                nc.sync.dma_start(dst[32 * q : 32 * q + 4, :].bitcast(I32), src[0, 4 * q : 4 * q + 4, :].bitcast(I32))
+
+        def load_weight_words(name, src):
+            raw = sb(name, [P, 2 * N], U8)
+            nc.sync.dma_start(raw[:].bitcast(I32), src[0].bitcast(I32))
+            return raw
+
+        def cols(lst, lo, hi):
+            return lst[:, lo // 16 : hi // 16]
+
+        x_scale_table = sb("x_scale_table", [P, TOKENS], U8)
+        nc.vector.memset(x_scale_table[:].bitcast(I32), 0)
+        raw_scales = {}
+        for name in ("w3", "w1", "w2"):
+            raw_scales[name] = sb(name + "_raw_scales", [P, N], U8)
+            nc.vector.memset(raw_scales[name][:].bitcast(I32), 0)
+
+        x_word_table = sb("x_word_table", [P, TOKENS], I32)
+        nc.sync.dma_start(x_word_table[:], x_words[0].rearrange("p n t -> p (n t)").bitcast(I32))
+        three_list = load_list("three_list", three)
+        load_scale_rows(x_scale_table, x_scales)
+        raw_words = {"w3": load_weight_words("w3_raw_words", w3_words)}
+        gb_col = load_column("gb_col", gb, nc.sync)
+        load_scale_rows(raw_scales["w3"], w3_scales)
+        n4_list = load_list("n4_list", n4)
+        offs_list = load_list("offs_list", offs)
+        raw_words["w1"] = load_weight_words("w1_raw_words", w1_words)
+        ga_col = load_column("ga_col", ga, nc.sync)
+        load_scale_rows(raw_scales["w1"], w1_scales)
+        two_list = load_list("two_list", two)
+        raw_words["w2"] = load_weight_words("w2_raw_words", w2_words)
+        load_scale_rows(raw_scales["w2"], w2_scales)
+        n1_list = load_list("n1_list", n1)
+        n2_list = load_list("n2_list", n2)
+        n3_list = load_list("n3_list", n3)
+        n5_list = load_list("n5_list", n5)
+        n6_list = load_list("n6_list", n6)
+        sl_col = load_column("sl_col", sl, nc.sync)
+        th_col = load_column("th_col", th, nc.sync)
+        sl2_col = load_column("sl2_col", sl2, nc.sync)
+        th2_col = load_column("th2_col", th2, nc.sync)
+
+        def first_layer(name, lst):
+            words = sb(name + "_words", [P, 2 * N], U8)
+            nc.scalar.copy(
+                words[:].bitcast(U16).rearrange("p (t m) -> p t m", t=PACK),
+                raw_words[name][:].bitcast(U16).rearrange("p (m t) -> p t m", t=PACK),
+            )
+            picked_scales = sb(name + "_picked_scales", [P, N], U8)
+            nc.vector.tensor_copy(picked_scales[:], x_scale_table[:].indirect(lst[:]))
+            picked_words = sb(name + "_picked_words", [P, N], U32)
+            nc.vector.tensor_copy(picked_words[:], x_word_table[:].bitcast(U32).indirect(lst[:]))
+            scales = sb(name + "_scales", [P, N], U8)
+            nc.vector.tensor_copy(
+                scales[:].rearrange("p (t m) -> p t m", t=PACK),
+                raw_scales[name][:].rearrange("p (m t) -> p t m", t=PACK),
+            )
+            banks = []
+            for t in range(PACK):
+                bank = psum.tile([P, N], F32, name="bank")
+                nc.tensor.matmul_mx(
+                    bank[:],
+                    lhsT=words[:, 2 * P * t : 2 * P * (t + 1)].bitcast(FP4X4),
+                    lhsT_scale=scales[:, P * t : P * (t + 1)],
+                    rhs=picked_words[:].bitcast(FP8X4),
+                    rhs_scale=picked_scales[:],
+                    start=True,
+                    stop=True,
+                )
+                banks.append(bank)
+            return banks
+
+        def scaled_rows(name, bank, factor, on_scalar):
+            rows = sb(name, [P, N], F32)
+            if on_scalar:
+                nc.scalar.activation(rows[:], bank[:], ACT.Copy, scale=factor)
+            else:
+                nc.vector.tensor_scalar(rows[:], bank[:], factor, None, ALU.mult)
+            return rows
+
+        def fetch(dst, rows, lst, lo, hi, on_vector):
+            if on_vector:
+                nc.vector.tensor_copy(dst, rows[:].indirect(cols(lst, lo, hi)))
+            else:
+                nc.scalar.activation(dst, rows[:].indirect(cols(lst, lo, hi)), ACT.Copy)
+
+        b_banks = first_layer("w3", three_list)
+        b_rows = [scaled_rows("b_rows%d" % t, b_banks[t], gb_col[:, t : t + 1], t == 0) for t in range(PACK)]
+        members = [sb("members%d" % t, [P, PACK * N], BF16) for t in range(PACK)]
+
+        def fetch_members(t):
+            for lo in range(0, PACK * N, PIECE):
+                on_vector = t == PACK - 1 and lo >= PACK * N - MEMBER_PIECES_ON_VECTOR * PIECE
+                fetch(members[t][:, lo : lo + PIECE], b_rows[t], n4_list, lo, lo + PIECE, on_vector)
+
+        z2_upper = sb("z2_upper", [P, PACK, N], BF16)
+        z2_lower = sb("z2_lower", [P, PACK, N], BF16)
+
+        def clamp_parts(t):
+            four = members[t][:].rearrange("p (v u e) -> p v u e", u=2, e=2)
+            hi = sb("hi%d" % t, [P, N, 2], BF16)
+            lo = sb("lo%d" % t, [P, N, 2], BF16)
+            nc.vector.tensor_tensor(hi[:], four[:, :, 0, :], four[:, :, 1, :], ALU.max)
+            nc.vector.tensor_tensor(lo[:], four[:, :, 0, :], four[:, :, 1, :], ALU.min)
+            largest = sb("largest%d" % t, [P, N], BF16)
+            nc.vector.tensor_tensor(largest[:], hi[:, :, 0], hi[:, :, 1], ALU.max)
+            nc.vector.tensor_tensor(z2_lower[:, t, :], lo[:, :, 0], lo[:, :, 1], ALU.min)
+            nc.vector.scalar_tensor_tensor(z2_upper[:, t, :], b_rows[t][:], 1.5, largest[:], ALU.mult, ALU.min)
+
+        fetch_members(0)
+        ga_abs = sb("ga_abs", [P, PACK], F32)
+        ga_sign = sb("ga_sign", [P, PACK], F32)
+        nc.vector.scalar_tensor_tensor(ga_abs[:], ga_col[:], -1.0, ga_col[:], ALU.mult, ALU.max)
+        nc.scalar.activation(ga_sign[:], ga_col[:], ACT.Sign)
+        y_banks = first_layer("w1", offs_list)
+        y_rows = [scaled_rows("y_rows%d" % t, y_banks[t], ga_abs[:, t : t + 1], False) for t in range(PACK)]
+        fetch_members(1)
+        d_banks = first_layer("w2", two_list)
+        d_rows = [scaled_rows("d_rows%d" % t, d_banks[t], ga_abs[:, t : t + 1], False) for t in range(PACK)]
+
+        bias1 = sb("bias1", [P, PACK], F32)
+        scale2 = sb("scale2", [P, PACK], F32)
+        bias2 = sb("bias2", [P, PACK], F32)
+        nc.vector.scalar_tensor_tensor(bias1[:], sl_col[:], -1.0, th_col[:], ALU.mult, ALU.mult)
+        nc.vector.tensor_scalar(scale2[:], sl2_col[:], -1.0, None, ALU.mult)
+        nc.vector.tensor_tensor(bias2[:], sl2_col[:], th2_col[:], ALU.mult)
+
+        clamp_parts(0)
+        fetch_members(2)
+        clamp_parts(1)
+        fetch_members(3)
+        clamp_parts(2)
+        clamp_parts(3)
+
+        z2_bf = sb("z2_bf", [P, N, PACK], BF16)
+        nc.vector.tensor_tensor(
+            z2_bf[:].rearrange("p (c i) t -> p c t i", i=4),
+            z2_upper[:].rearrange("p t (c i) -> p c t i", i=4),
+            z2_lower[:].rearrange("p t (c i) -> p c t i", i=4),
+            ALU.max,
+        )
+        z2_codes = sb("z2_codes", [P, N], U32)
+        z2_scales = sb("z2_scales", [P, N], U8)
+        nc.vector.quantize_mx(z2_codes[:].bitcast(FP8X4), z2_scales[:], z2_bf[:].rearrange("p v t -> p (v t)"))
+
+        y_at_n1 = sb("y_at_n1", [P, PACK, N], F32)
+        d_at_n2 = sb("d_at_n2", [P, PACK, N], BF16)
+        d_at_n3 = sb("d_at_n3", [P, PACK, N], BF16)
+        y_less = sb("y_less", [P, PACK, N], BF16)
+        capped = sb("capped", [P, PACK, N], BF16)
+        held = sb("held", [P, PACK, N], BF16)
+        z_bf = sb("z_bf", [P, PACK, P, PACK], BF16)
+        for lo, hi in Z_PIECES:
+            for t in range(PACK):
+                fetch(y_at_n1[:, t, lo:hi], y_rows[t], n1_list, lo, hi, False)
+            for t in range(PACK):
+                fetch(d_at_n2[:, t, lo:hi], d_rows[t], n2_list, lo, hi, False)
+            for t in range(PACK):
+                fetch(d_at_n3[:, t, lo:hi], d_rows[t], n3_list, lo, hi, False)
+            for t in range(PACK):
+                nc.vector.scalar_tensor_tensor(
+                    y_less[:, t, lo:hi], y_at_n1[:, t, lo:hi], -0.5, y_rows[t][:, lo:hi], ALU.mult, ALU.add
+                )
+            nc.vector.tensor_tensor(capped[:, :, lo:hi], y_less[:, :, lo:hi], d_at_n2[:, :, lo:hi], ALU.min)
+            nc.vector.tensor_tensor(held[:, :, lo:hi], capped[:, :, lo:hi], d_at_n3[:, :, lo:hi], ALU.max)
+            m = (hi - lo) // PACK
+            nc.vector.tensor_tensor(
+                z_bf[:, :, lo // PACK : hi // PACK, :],
+                held[:, :, lo:hi].rearrange("p t (m u) -> p u m t", u=PACK),
+                ga_sign[:].unsqueeze(1).unsqueeze(1).to_broadcast([P, PACK, m, PACK]),
+                ALU.mult,
+            )
+
+        z_codes = sb("z_codes", [P, N], U32)
+        z_scales = sb("z_scales", [P, N], U8)
+        s_banks = []
+        for u in range(PACK):
+            at = slice(P * u, P * (u + 1))
+            nc.vector.quantize_mx(z_codes[:, at].bitcast(FP8X4), z_scales[:, at], z_bf[:, u].rearrange("p m t -> p (m t)"))
+            bank = psum.tile([P, N], F32, name="bank")
+            nc.tensor.matmul_mx(
+                bank[:],
+                lhsT=z_codes[:, at].bitcast(FP8X4),
+                lhsT_scale=z_scales[:, at],
+                rhs=z2_codes[:].bitcast(FP8X4),
+                rhs_scale=z2_scales[:],
+                start=True,
+                stop=True,
+            )
+            s_banks.append(bank)
+        s_rows = [scaled_rows("s_rows%d" % u, s_banks[u], 0.0625, False) for u in range(PACK)]
+
+        gate1 = sb("gate1", [P, PACK, N], F32)
+        gate2 = sb("gate2", [P, PACK, N], F32)
+        half_gated = sb("half_gated", [P, PACK, N], F32)
+        result = sb("result", [P, PACK, N], F32)
+        result_bf = sb("result_bf", [P, N, PACK], BF16)
+        result_codes = sb("result_codes", [P, N], I32)
+        result_scales = sb("result_scales", [P, N], U8)
+        out_rows = out_0.rearrange("(p u) v -> p u v", u=PACK)
+        out_words = out_1[0].rearrange("p v r -> p (v r)").bitcast(I32)
+        for lo, hi in OUT_PIECES:
+            for u in range(PACK):
+                one = slice(u, u + 1)
+                nc.scalar.activation(
+                    gate1[:, u, lo:hi], s_rows[u][:].indirect(cols(n5_list, lo, hi)), ACT.Sigmoid,
+                    bias=bias1[:, one], scale=sl_col[:, one],
+                )
+                nc.scalar.activation(
+                    gate2[:, u, lo:hi], s_rows[u][:].indirect(cols(n6_list, lo, hi)), ACT.Sigmoid,
+                    bias=bias2[:, one], scale=scale2[:, one],
+                )
+                nc.vector.scalar_tensor_tensor(
+                    half_gated[:, u, lo:hi], s_rows[u][:, lo:hi], 2.0, gate1[:, u, lo:hi], ALU.mult, ALU.mult
+                )
+                nc.vector.tensor_tensor(result[:, u, lo:hi], half_gated[:, u, lo:hi], gate2[:, u, lo:hi], ALU.mult)
+            nc.sync.dma_start(out_rows[:, :, lo:hi], result[:, :, lo:hi])
+            nc.vector.tensor_copy(
+                result_bf[:, lo:hi, :].rearrange("p (c i) u -> p c u i", i=4),
+                result[:, :, lo:hi].rearrange("p u (c i) -> p c u i", i=4),
+            )
+            nc.vector.quantize_mx(
+                result_codes[:, lo:hi].bitcast(FP8X4), result_scales[:, lo:hi],
+                result_bf[:, lo:hi, :].rearrange("p v u -> p (v u)"),
+            )
+            nc.sync.dma_start(out_words[:, lo:hi], result_codes[:, lo:hi])
+        for q in range(4):
+            queue = nc.scalar if q % 2 == 0 else nc.sync
+            queue.dma_start(out_2[0, 4 * q : 4 * q + 4, :].bitcast(I32), result_scales[32 * q : 32 * q + 4, :].bitcast(I32))

@@ -1,6 +1,7 @@
 from contextlib import ExitStack
 
 import concourse.mybir as mybir
+from concourse.masks import make_identity
 
 FLOPS = 4 * 2 * 512 * 512 * 512
 
@@ -19,10 +20,11 @@ P = 128
 PACK = 4
 N = 512
 TOKENS = 2048
+RUN = 8
 PIECE = 256
 Z_PIECES = ((0, 256), (256, 384), (384, 512))
 OUT_PIECES = ((0, 256), (256, 384), (384, 512))
-MEMBER_PIECES_ON_VECTOR = 2
+MEMBER_PIECES_ON_VECTOR = 7
 
 
 def tile_picked_twkclampbgclipecr_none_po_kernel(
@@ -34,8 +36,8 @@ def tile_picked_twkclampbgclipecr_none_po_kernel(
         keep = ctx.enter_context(tc.tile_pool(name="keep", bufs=1))
         psum = ctx.enter_context(tc.psum_pool(name="psum", bufs=8))
 
-        def sb(name, shape, dtype):
-            return keep.tile(shape, dtype, name=name, align_bytes=64)
+        def sb(name, shape, dtype, tag=None):
+            return keep.tile(shape, dtype, name=name, tag=tag or name, align_bytes=64)
 
         def load_list(name, src):
             lst = keep.tile(list(src.shape), U16, name=name)
@@ -47,9 +49,9 @@ def tile_picked_twkclampbgclipecr_none_po_kernel(
             queue.dma_start(col[:], src.rearrange("(p t) o -> p (t o)", t=PACK))
             return col
 
-        def load_scale_rows(dst, src):
+        def load_scale_rows(dst, src, queues):
             for q in range(4):
-                nc.sync.dma_start(dst[32 * q : 32 * q + 4, :].bitcast(I32), src[0, 4 * q : 4 * q + 4, :].bitcast(I32))
+                queues[q].dma_start(dst[32 * q : 32 * q + 4, :].bitcast(I32), src[0, 4 * q : 4 * q + 4, :].bitcast(I32))
 
         def load_weight_words(name, src):
             raw = sb(name, [P, 2 * N], U8)
@@ -66,21 +68,29 @@ def tile_picked_twkclampbgclipecr_none_po_kernel(
             raw_scales[name] = sb(name + "_raw_scales", [P, N], U8)
             nc.vector.memset(raw_scales[name][:].bitcast(I32), 0)
 
+        gain_rows = sb("gain_rows", [P, P], F32)
+        nc.gpsimd.memset(gain_rows[:], 0.0)
+        for row, src in ((PACK, gb), (0, ga)):
+            nc.gpsimd.dma_start(
+                gain_rows[row : row + PACK, :].rearrange("t (q e) -> t q e", e=RUN),
+                src.rearrange("(q t e) o -> t q (e o)", t=PACK, e=RUN),
+            )
+        identity = sb("identity", [P, P], F32)
+        make_identity(nc, identity[:])
+
         x_word_table = sb("x_word_table", [P, TOKENS], I32)
         nc.sync.dma_start(x_word_table[:], x_words[0].rearrange("p n t -> p (n t)").bitcast(I32))
         three_list = load_list("three_list", three)
-        load_scale_rows(x_scale_table, x_scales)
+        load_scale_rows(x_scale_table, x_scales, [nc.sync] * 4)
         raw_words = {"w3": load_weight_words("w3_raw_words", w3_words)}
-        gb_col = load_column("gb_col", gb, nc.sync)
-        load_scale_rows(raw_scales["w3"], w3_scales)
+        load_scale_rows(raw_scales["w3"], w3_scales, [nc.sync] * 4)
+        raw_words["w1"] = load_weight_words("w1_raw_words", w1_words)
+        raw_words["w2"] = load_weight_words("w2_raw_words", w2_words)
         n4_list = load_list("n4_list", n4)
         offs_list = load_list("offs_list", offs)
-        raw_words["w1"] = load_weight_words("w1_raw_words", w1_words)
-        ga_col = load_column("ga_col", ga, nc.sync)
-        load_scale_rows(raw_scales["w1"], w1_scales)
         two_list = load_list("two_list", two)
-        raw_words["w2"] = load_weight_words("w2_raw_words", w2_words)
-        load_scale_rows(raw_scales["w2"], w2_scales)
+        load_scale_rows(raw_scales["w1"], w1_scales, [nc.sync] * 4)
+        load_scale_rows(raw_scales["w2"], w2_scales, [nc.sync] * 4)
         n1_list = load_list("n1_list", n1)
         n2_list = load_list("n2_list", n2)
         n3_list = load_list("n3_list", n3)
@@ -91,21 +101,27 @@ def tile_picked_twkclampbgclipecr_none_po_kernel(
         sl2_col = load_column("sl2_col", sl2, nc.sync)
         th2_col = load_column("th2_col", th2, nc.sync)
 
+        dealt_words = {}
+        dealt_scales = {}
+        for name in ("w3", "w1", "w2"):
+            dealt_words[name] = sb(name + "_words", [P, 2 * N], U8)
+            dealt_scales[name] = sb(name + "_scales", [P, N], U8)
+            for dealt, raw, width in (
+                (dealt_words[name], raw_words[name], RUN // 2),
+                (dealt_scales[name], raw_scales[name], RUN // 4),
+            ):
+                nc.scalar.copy(
+                    dealt[:].bitcast(U32).rearrange("p (t q e) -> p t q e", t=PACK, e=width),
+                    raw[:].bitcast(U32).rearrange("p (q t e) -> p t q e", t=PACK, e=width),
+                )
+
         def first_layer(name, lst):
-            words = sb(name + "_words", [P, 2 * N], U8)
-            nc.scalar.copy(
-                words[:].bitcast(U16).rearrange("p (t m) -> p t m", t=PACK),
-                raw_words[name][:].bitcast(U16).rearrange("p (m t) -> p t m", t=PACK),
-            )
-            picked_scales = sb(name + "_picked_scales", [P, N], U8)
-            nc.vector.tensor_copy(picked_scales[:], x_scale_table[:].indirect(lst[:]))
+            words = dealt_words[name]
+            scales = dealt_scales[name]
             picked_words = sb(name + "_picked_words", [P, N], U32)
             nc.vector.tensor_copy(picked_words[:], x_word_table[:].bitcast(U32).indirect(lst[:]))
-            scales = sb(name + "_scales", [P, N], U8)
-            nc.vector.tensor_copy(
-                scales[:].rearrange("p (t m) -> p t m", t=PACK),
-                raw_scales[name][:].rearrange("p (m t) -> p t m", t=PACK),
-            )
+            picked_scales = sb(name + "_picked_scales", [P, N], U8)
+            nc.vector.tensor_copy(picked_scales[:], x_scale_table[:].indirect(lst[:]))
             banks = []
             for t in range(PACK):
                 bank = psum.tile([P, N], F32, name="bank")
@@ -135,53 +151,73 @@ def tile_picked_twkclampbgclipecr_none_po_kernel(
             else:
                 nc.scalar.activation(dst, rows[:].indirect(cols(lst, lo, hi)), ACT.Copy)
 
+        gain_bank = psum.tile([P, P], F32, name="bank")
+        nc.tensor.transpose(gain_bank[:], gain_rows[:], identity[:])
+        gains = sb("gains", [P, 2 * PACK], F32)
+        nc.scalar.copy(gains[:], gain_bank[:, : 2 * PACK])
+        ga_col = gains[:, :PACK]
+        gb_col = gains[:, PACK:]
+
         b_banks = first_layer("w3", three_list)
         b_rows = [scaled_rows("b_rows%d" % t, b_banks[t], gb_col[:, t : t + 1], t == 0) for t in range(PACK)]
-        members = [sb("members%d" % t, [P, PACK * N], BF16) for t in range(PACK)]
+        first_members = sb("first_members", [P, 1, PACK * N], BF16, "w1_raw_scales")
+        later_members = sb("later_members", [P, PACK - 1, PACK * N], BF16, "w2_raw_scales")
+
+        def members(t_lo, t_hi):
+            return first_members[:] if t_lo == 0 else later_members[:, t_lo - 1 : t_hi - 1, :]
 
         def fetch_members(t):
             for lo in range(0, PACK * N, PIECE):
                 on_vector = t == PACK - 1 and lo >= PACK * N - MEMBER_PIECES_ON_VECTOR * PIECE
-                fetch(members[t][:, lo : lo + PIECE], b_rows[t], n4_list, lo, lo + PIECE, on_vector)
+                fetch(members(t, t + 1)[:, 0, lo : lo + PIECE], b_rows[t], n4_list, lo, lo + PIECE, on_vector)
 
         z2_upper = sb("z2_upper", [P, PACK, N], BF16)
         z2_lower = sb("z2_lower", [P, PACK, N], BF16)
 
-        def clamp_parts(t):
-            four = members[t][:].rearrange("p (v u e) -> p v u e", u=2, e=2)
-            hi = sb("hi%d" % t, [P, N, 2], BF16)
-            lo = sb("lo%d" % t, [P, N, 2], BF16)
+        def clamp_parts(t_lo, t_hi):
+            width = (t_hi - t_lo) * N
+            four = members(t_lo, t_hi).rearrange("p t (v u e) -> p (t v) u e", u=2, e=2)
+            hi = sb("hi%d" % t_lo, [P, width, 2], BF16, "w2_scales")
+            lo = sb("lo%d" % t_lo, [P, width, 2], BF16, "w2_words")
             nc.vector.tensor_tensor(hi[:], four[:, :, 0, :], four[:, :, 1, :], ALU.max)
             nc.vector.tensor_tensor(lo[:], four[:, :, 0, :], four[:, :, 1, :], ALU.min)
-            largest = sb("largest%d" % t, [P, N], BF16)
+            largest = sb("largest%d" % t_lo, [P, width], BF16)
             nc.vector.tensor_tensor(largest[:], hi[:, :, 0], hi[:, :, 1], ALU.max)
-            nc.vector.tensor_tensor(z2_lower[:, t, :], lo[:, :, 0], lo[:, :, 1], ALU.min)
-            nc.vector.scalar_tensor_tensor(z2_upper[:, t, :], b_rows[t][:], 1.5, largest[:], ALU.mult, ALU.min)
+            nc.vector.tensor_tensor(
+                z2_lower[:, t_lo:t_hi, :].rearrange("p t v -> p (t v)"), lo[:, :, 0], lo[:, :, 1], ALU.min
+            )
+            for t in range(t_lo, t_hi):
+                nc.vector.scalar_tensor_tensor(
+                    z2_upper[:, t, :], b_rows[t][:], 1.5, largest[:, N * (t - t_lo) : N * (t - t_lo + 1)], ALU.mult, ALU.min
+                )
 
         fetch_members(0)
         ga_abs = sb("ga_abs", [P, PACK], F32)
+        ga_step = sb("ga_step", [P, PACK], F32)
         ga_sign = sb("ga_sign", [P, PACK], F32)
-        nc.vector.scalar_tensor_tensor(ga_abs[:], ga_col[:], -1.0, ga_col[:], ALU.mult, ALU.max)
-        nc.scalar.activation(ga_sign[:], ga_col[:], ACT.Sign)
+        nc.gpsimd.tensor_scalar(ga_step[:], ga_col, 0.0, 2.0, ALU.is_ge, ALU.mult)
+        nc.gpsimd.tensor_scalar(ga_sign[:], ga_step[:], 1.0, -1.0, ALU.mult, ALU.add)
+        nc.gpsimd.tensor_tensor(ga_abs[:], ga_col, ga_sign[:], ALU.mult)
         y_banks = first_layer("w1", offs_list)
         y_rows = [scaled_rows("y_rows%d" % t, y_banks[t], ga_abs[:, t : t + 1], False) for t in range(PACK)]
         fetch_members(1)
         d_banks = first_layer("w2", two_list)
         d_rows = [scaled_rows("d_rows%d" % t, d_banks[t], ga_abs[:, t : t + 1], False) for t in range(PACK)]
 
+        neg_th = sb("neg_th", [P, PACK], F32)
         bias1 = sb("bias1", [P, PACK], F32)
         scale2 = sb("scale2", [P, PACK], F32)
         bias2 = sb("bias2", [P, PACK], F32)
-        nc.vector.scalar_tensor_tensor(bias1[:], sl_col[:], -1.0, th_col[:], ALU.mult, ALU.mult)
-        nc.vector.tensor_scalar(scale2[:], sl2_col[:], -1.0, None, ALU.mult)
-        nc.vector.tensor_tensor(bias2[:], sl2_col[:], th2_col[:], ALU.mult)
+        nc.gpsimd.tensor_scalar(neg_th[:], th_col[:], -1.0, 0.0, ALU.mult, ALU.add)
+        nc.gpsimd.tensor_tensor(bias1[:], sl_col[:], neg_th[:], ALU.mult)
+        nc.gpsimd.tensor_scalar(scale2[:], sl2_col[:], -1.0, 0.0, ALU.mult, ALU.add)
+        nc.gpsimd.tensor_tensor(bias2[:], sl2_col[:], th2_col[:], ALU.mult)
 
-        clamp_parts(0)
         fetch_members(2)
-        clamp_parts(1)
         fetch_members(3)
-        clamp_parts(2)
-        clamp_parts(3)
+        clamp_parts(0, 1)
+        clamp_parts(1, 3)
+        clamp_parts(3, 4)
 
         z2_bf = sb("z2_bf", [P, N, PACK], BF16)
         nc.vector.tensor_tensor(
@@ -201,45 +237,55 @@ def tile_picked_twkclampbgclipecr_none_po_kernel(
         capped = sb("capped", [P, PACK, N], BF16)
         held = sb("held", [P, PACK, N], BF16)
         z_bf = sb("z_bf", [P, PACK, P, PACK], BF16)
+
+        def sign_and_deal(lo, hi, u_lo, u_hi):
+            dealt = held[:, :, lo:hi].rearrange("p t (m u) -> p u m t", u=PACK)
+            signs = ga_sign[:].unsqueeze(1).unsqueeze(1).to_broadcast([P, u_hi - u_lo, (hi - lo) // PACK, PACK])
+            nc.vector.tensor_tensor(z_bf[:, u_lo:u_hi, lo // PACK : hi // PACK, :], dealt[:, u_lo:u_hi], signs, ALU.mult)
+
+        for t in range(PACK):
+            for lo in range(0, N, PIECE):
+                fetch(y_at_n1[:, t, lo : lo + PIECE], y_rows[t], n1_list, lo, lo + PIECE, False)
+            nc.vector.scalar_tensor_tensor(y_less[:, t, :], y_at_n1[:, t, :], -0.5, y_rows[t][:], ALU.mult, ALU.add)
+        for lo in range(0, N, PIECE):
+            for t in range(PACK):
+                fetch(d_at_n2[:, t, lo : lo + PIECE], d_rows[t], n2_list, lo, lo + PIECE, False)
+            at = slice(lo, lo + PIECE)
+            nc.vector.tensor_tensor(capped[:, :, at], y_less[:, :, at], d_at_n2[:, :, at], ALU.min)
         for lo, hi in Z_PIECES:
             for t in range(PACK):
-                fetch(y_at_n1[:, t, lo:hi], y_rows[t], n1_list, lo, hi, False)
-            for t in range(PACK):
-                fetch(d_at_n2[:, t, lo:hi], d_rows[t], n2_list, lo, hi, False)
-            for t in range(PACK):
                 fetch(d_at_n3[:, t, lo:hi], d_rows[t], n3_list, lo, hi, False)
-            for t in range(PACK):
-                nc.vector.scalar_tensor_tensor(
-                    y_less[:, t, lo:hi], y_at_n1[:, t, lo:hi], -0.5, y_rows[t][:, lo:hi], ALU.mult, ALU.add
-                )
-            nc.vector.tensor_tensor(capped[:, :, lo:hi], y_less[:, :, lo:hi], d_at_n2[:, :, lo:hi], ALU.min)
             nc.vector.tensor_tensor(held[:, :, lo:hi], capped[:, :, lo:hi], d_at_n3[:, :, lo:hi], ALU.max)
-            m = (hi - lo) // PACK
-            nc.vector.tensor_tensor(
-                z_bf[:, :, lo // PACK : hi // PACK, :],
-                held[:, :, lo:hi].rearrange("p t (m u) -> p u m t", u=PACK),
-                ga_sign[:].unsqueeze(1).unsqueeze(1).to_broadcast([P, PACK, m, PACK]),
-                ALU.mult,
-            )
+            if hi < N:
+                sign_and_deal(lo, hi, 0, PACK)
 
         z_codes = sb("z_codes", [P, N], U32)
         z_scales = sb("z_scales", [P, N], U8)
-        s_banks = []
+        s_rows = []
         for u in range(PACK):
+            if u < 2:
+                sign_and_deal(Z_PIECES[-1][0], N, u, 1 if u == 0 else PACK)
             at = slice(P * u, P * (u + 1))
             nc.vector.quantize_mx(z_codes[:, at].bitcast(FP8X4), z_scales[:, at], z_bf[:, u].rearrange("p m t -> p (m t)"))
-            bank = psum.tile([P, N], F32, name="bank")
-            nc.tensor.matmul_mx(
-                bank[:],
-                lhsT=z_codes[:, at].bitcast(FP8X4),
-                lhsT_scale=z_scales[:, at],
-                rhs=z2_codes[:].bitcast(FP8X4),
-                rhs_scale=z2_scales[:],
-                start=True,
-                stop=True,
-            )
-            s_banks.append(bank)
-        s_rows = [scaled_rows("s_rows%d" % u, s_banks[u], 0.0625, False) for u in range(PACK)]
+            rows = sb("s_rows%d" % u, [P, N], F32)
+            width = N // 2 if u == 0 else N
+            for lo in range(0, N, width):
+                part = slice(lo, lo + width)
+                bank = psum.tile([P, width], F32, name="bank")
+                nc.tensor.matmul_mx(
+                    bank[:],
+                    lhsT=z_codes[:, at].bitcast(FP8X4),
+                    lhsT_scale=z_scales[:, at],
+                    rhs=z2_codes[:, part].bitcast(FP8X4),
+                    rhs_scale=z2_scales[:, part],
+                    start=True,
+                    stop=True,
+                )
+                if lo > 0:
+                    nc.scalar.activation(rows[:, part], bank[:], ACT.Copy, scale=0.0625)
+                else:
+                    nc.vector.tensor_scalar(rows[:, part], bank[:], 0.0625, None, ALU.mult)
+            s_rows.append(rows)
 
         gate1 = sb("gate1", [P, PACK, N], F32)
         gate2 = sb("gate2", [P, PACK, N], F32)
@@ -251,20 +297,23 @@ def tile_picked_twkclampbgclipecr_none_po_kernel(
         out_rows = out_0.rearrange("(p u) v -> p u v", u=PACK)
         out_words = out_1[0].rearrange("p v r -> p (v r)").bitcast(I32)
         for lo, hi in OUT_PIECES:
+            if lo % PIECE == 0:
+                at = slice(lo, lo + PIECE)
+                for u in range(PACK):
+                    nc.scalar.activation(
+                        gate1[:, u, at], s_rows[u][:].indirect(cols(n5_list, lo, lo + PIECE)), ACT.Sigmoid,
+                        bias=bias1[:, u : u + 1], scale=sl_col[:, u : u + 1],
+                    )
+                    nc.vector.scalar_tensor_tensor(half_gated[:, u, at], s_rows[u][:, at], 2.0, gate1[:, u, at], ALU.mult, ALU.mult)
             for u in range(PACK):
-                one = slice(u, u + 1)
-                nc.scalar.activation(
-                    gate1[:, u, lo:hi], s_rows[u][:].indirect(cols(n5_list, lo, hi)), ACT.Sigmoid,
-                    bias=bias1[:, one], scale=sl_col[:, one],
-                )
                 nc.scalar.activation(
                     gate2[:, u, lo:hi], s_rows[u][:].indirect(cols(n6_list, lo, hi)), ACT.Sigmoid,
-                    bias=bias2[:, one], scale=scale2[:, one],
+                    bias=bias2[:, u : u + 1], scale=scale2[:, u : u + 1],
                 )
-                nc.vector.scalar_tensor_tensor(
-                    half_gated[:, u, lo:hi], s_rows[u][:, lo:hi], 2.0, gate1[:, u, lo:hi], ALU.mult, ALU.mult
+            for u_lo, u_hi in ((0, PACK - 1), (PACK - 1, PACK)) if hi == N else ((0, PACK),):
+                nc.vector.tensor_tensor(
+                    result[:, u_lo:u_hi, lo:hi], half_gated[:, u_lo:u_hi, lo:hi], gate2[:, u_lo:u_hi, lo:hi], ALU.mult
                 )
-                nc.vector.tensor_tensor(result[:, u, lo:hi], half_gated[:, u, lo:hi], gate2[:, u, lo:hi], ALU.mult)
             nc.sync.dma_start(out_rows[:, :, lo:hi], result[:, :, lo:hi])
             nc.vector.tensor_copy(
                 result_bf[:, lo:hi, :].rearrange("p (c i) u -> p c u i", i=4),

@@ -24,7 +24,7 @@ RUN = 8
 PIECE = 256
 Z_PIECES = ((0, 256), (256, 384), (384, 512))
 OUT_PIECES = ((0, 256), (256, 384), (384, 512))
-MEMBER_PIECES_ON_VECTOR = 7
+MEMBER_PIECES_ON_VECTOR = 4
 
 
 def tile_picked_twkclampbgclipecr_none_po_kernel(
@@ -198,6 +198,8 @@ def tile_picked_twkclampbgclipecr_none_po_kernel(
         nc.gpsimd.tensor_scalar(ga_step[:], ga_col, 0.0, 2.0, ALU.is_ge, ALU.mult)
         nc.gpsimd.tensor_scalar(ga_sign[:], ga_step[:], 1.0, -1.0, ALU.mult, ALU.add)
         nc.gpsimd.tensor_tensor(ga_abs[:], ga_col, ga_sign[:], ALU.mult)
+        ga_sign_bf = sb("ga_sign_bf", [P, PACK], BF16)
+        nc.gpsimd.tensor_copy(ga_sign_bf[:], ga_sign[:])
         y_banks = first_layer("w1", offs_list)
         y_rows = [scaled_rows("y_rows%d" % t, y_banks[t], ga_abs[:, t : t + 1], False) for t in range(PACK)]
         fetch_members(1)
@@ -219,12 +221,11 @@ def tile_picked_twkclampbgclipecr_none_po_kernel(
         clamp_parts(1, 3)
         clamp_parts(3, 4)
 
+        z2_planes = sb("z2_planes", [P, PACK, N], BF16)
+        nc.vector.tensor_tensor(z2_planes[:], z2_upper[:], z2_lower[:], ALU.max)
         z2_bf = sb("z2_bf", [P, N, PACK], BF16)
-        nc.vector.tensor_tensor(
-            z2_bf[:].rearrange("p (c i) t -> p c t i", i=4),
-            z2_upper[:].rearrange("p t (c i) -> p c t i", i=4),
-            z2_lower[:].rearrange("p t (c i) -> p c t i", i=4),
-            ALU.max,
+        nc.vector.tensor_copy(
+            z2_bf[:].rearrange("p (c i) t -> p c t i", i=4), z2_planes[:].rearrange("p t (c i) -> p c t i", i=4)
         )
         z2_codes = sb("z2_codes", [P, N], U32)
         z2_scales = sb("z2_scales", [P, N], U8)
@@ -238,10 +239,18 @@ def tile_picked_twkclampbgclipecr_none_po_kernel(
         held = sb("held", [P, PACK, N], BF16)
         z_bf = sb("z_bf", [P, PACK, P, PACK], BF16)
 
-        def sign_and_deal(lo, hi, u_lo, u_hi):
-            dealt = held[:, :, lo:hi].rearrange("p t (m u) -> p u m t", u=PACK)
-            signs = ga_sign[:].unsqueeze(1).unsqueeze(1).to_broadcast([P, u_hi - u_lo, (hi - lo) // PACK, PACK])
-            nc.vector.tensor_tensor(z_bf[:, u_lo:u_hi, lo // PACK : hi // PACK, :], dealt[:, u_lo:u_hi], signs, ALU.mult)
+        unsigned = sb("unsigned", [P, PACK, P, PACK], BF16)
+
+        def deal(lo, hi):
+            nc.vector.tensor_copy(
+                unsigned[:, :, lo // PACK : hi // PACK, :].rearrange("p u (c i) t -> p c u i t", i=2),
+                held[:, :, lo:hi].rearrange("p t (c i u) -> p c u i t", i=2, u=PACK),
+            )
+
+        def give_sign(lo, hi, u_lo, u_hi):
+            at = slice(lo // PACK, hi // PACK)
+            signs = ga_sign_bf[:].unsqueeze(1).unsqueeze(1).to_broadcast([P, u_hi - u_lo, (hi - lo) // PACK, PACK])
+            nc.vector.tensor_tensor(z_bf[:, u_lo:u_hi, at, :], unsigned[:, u_lo:u_hi, at, :], signs, ALU.mult)
 
         for t in range(PACK):
             for lo in range(0, N, PIECE):
@@ -256,15 +265,16 @@ def tile_picked_twkclampbgclipecr_none_po_kernel(
             for t in range(PACK):
                 fetch(d_at_n3[:, t, lo:hi], d_rows[t], n3_list, lo, hi, False)
             nc.vector.tensor_tensor(held[:, :, lo:hi], capped[:, :, lo:hi], d_at_n3[:, :, lo:hi], ALU.max)
+            deal(lo, hi)
             if hi < N:
-                sign_and_deal(lo, hi, 0, PACK)
+                give_sign(lo, hi, 0, PACK)
 
         z_codes = sb("z_codes", [P, N], U32)
         z_scales = sb("z_scales", [P, N], U8)
         s_rows = []
         for u in range(PACK):
             if u < 2:
-                sign_and_deal(Z_PIECES[-1][0], N, u, 1 if u == 0 else PACK)
+                give_sign(Z_PIECES[-1][0], N, u, 1 if u == 0 else PACK)
             at = slice(P * u, P * (u + 1))
             nc.vector.quantize_mx(z_codes[:, at].bitcast(FP8X4), z_scales[:, at], z_bf[:, u].rearrange("p m t -> p (m t)"))
             rows = sb("s_rows%d" % u, [P, N], F32)

@@ -61,6 +61,11 @@ def tile_picked_twkclampbgclipecr_none_po_kernel(
         def cols(lst, lo, hi):
             return lst[:, lo // 16 : hi // 16]
 
+        warm_in = sb("warm_in", [P, 1], F32)
+        warm_out = sb("warm_out", [P, 1], F32)
+        nc.vector.memset(warm_in[:], 0.0)
+        nc.scalar.activation(warm_out[:], warm_in[:], ACT.Sigmoid)
+
         x_scale_table = sb("x_scale_table", [P, TOKENS], U8)
         nc.vector.memset(x_scale_table[:].bitcast(I32), 0)
         raw_scales = {}

@@ -18,13 +18,14 @@ ACT = mybir.ActivationFunctionType
 
 P = 128
 PACK = 4
+QUADRANTS = 4
 N = 512
 TOKENS = 2048
+MEMBERS = 4 * N
 RUN = 8
-PIECE = 256
-Z_PIECES = ((0, 256), (256, 384), (384, 512))
-OUT_PIECES = ((0, 256), (256, 384), (384, 512))
-MEMBER_PIECES_ON_VECTOR = 4
+HALF = N // 2
+PIECES = ((0, 256), (256, 384), (384, 512))
+MEMBERS_ON_VECTOR = 1152
 
 
 def tile_picked_twkclampbgclipecr_none_po_kernel(
@@ -36,104 +37,104 @@ def tile_picked_twkclampbgclipecr_none_po_kernel(
         keep = ctx.enter_context(tc.tile_pool(name="keep", bufs=1))
         psum = ctx.enter_context(tc.psum_pool(name="psum", bufs=8))
 
-        def sb(name, shape, dtype, tag=None):
-            return keep.tile(shape, dtype, name=name, tag=tag or name, align_bytes=64)
+        def sbuf(name, shape, dtype, reuses=None):
+            return keep.tile(shape, dtype, name=name, tag=reuses or name, align_bytes=64)
 
         def load_list(name, src):
             lst = keep.tile(list(src.shape), U16, name=name)
             nc.sync.dma_start(lst[:], src)
             return lst
 
-        def load_column(name, src, queue):
-            col = sb(name, [P, PACK], F32)
-            queue.dma_start(col[:], src.rearrange("(p t) o -> p (t o)", t=PACK))
+        def load_by_slab(name, src):
+            col = sbuf(name, [P, PACK], F32)
+            nc.sync.dma_start(col[:], src.rearrange("(p u) o -> p (u o)", u=PACK))
             return col
 
-        def load_scale_rows(dst, src, queues):
-            for q in range(4):
-                queues[q].dma_start(dst[32 * q : 32 * q + 4, :].bitcast(I32), src[0, 4 * q : 4 * q + 4, :].bitcast(I32))
+        def load_scale_rows(dst, src):
+            for quad in range(QUADRANTS):
+                nc.sync.dma_start(
+                    dst[32 * quad : 32 * quad + 4, :].bitcast(I32), src[0, 4 * quad : 4 * quad + 4, :].bitcast(I32)
+                )
 
         def load_weight_words(name, src):
-            raw = sb(name, [P, 2 * N], U8)
+            raw = sbuf(name, [P, 2 * N], U8)
             nc.sync.dma_start(raw[:].bitcast(I32), src[0].bitcast(I32))
             return raw
 
-        def cols(lst, lo, hi):
+        def entries(lst, lo, hi):
             return lst[:, lo // 16 : hi // 16]
 
-        warm_in = sb("warm_in", [P, 1], F32)
-        warm_out = sb("warm_out", [P, 1], F32)
+        warm_in = sbuf("warm_in", [P, 1], F32)
+        warm_out = sbuf("warm_out", [P, 1], F32)
         nc.vector.memset(warm_in[:], 0.0)
         nc.scalar.activation(warm_out[:], warm_in[:], ACT.Sigmoid)
 
-        x_scale_table = sb("x_scale_table", [P, TOKENS], U8)
+        x_scale_table = sbuf("x_scale_table", [P, TOKENS], U8)
         nc.vector.memset(x_scale_table[:].bitcast(I32), 0)
         raw_scales = {}
         for name in ("w3", "w1", "w2"):
-            raw_scales[name] = sb(name + "_raw_scales", [P, N], U8)
+            raw_scales[name] = sbuf(name + "_raw_scales", [P, N], U8)
             nc.vector.memset(raw_scales[name][:].bitcast(I32), 0)
 
-        gain_rows = sb("gain_rows", [P, P], F32)
+        gain_rows = sbuf("gain_rows", [P, P], F32)
         nc.gpsimd.memset(gain_rows[:], 0.0)
         for row, src in ((PACK, gb), (0, ga)):
             nc.gpsimd.dma_start(
                 gain_rows[row : row + PACK, :].rearrange("t (q e) -> t q e", e=RUN),
                 src.rearrange("(q t e) o -> t q (e o)", t=PACK, e=RUN),
             )
-        identity = sb("identity", [P, P], F32)
+        identity = sbuf("identity", [P, P], F32)
         make_identity(nc, identity[:])
 
-        x_word_table = sb("x_word_table", [P, TOKENS], I32)
-        nc.sync.dma_start(x_word_table[:], x_words[0].rearrange("p n t -> p (n t)").bitcast(I32))
+        x_word_table = sbuf("x_word_table", [P, TOKENS], I32)
+        nc.sync.dma_start(x_word_table[:], x_words[0].rearrange("p n r -> p (n r)").bitcast(I32))
         three_list = load_list("three_list", three)
-        load_scale_rows(x_scale_table, x_scales, [nc.sync] * 4)
+        load_scale_rows(x_scale_table, x_scales)
         raw_words = {"w3": load_weight_words("w3_raw_words", w3_words)}
-        load_scale_rows(raw_scales["w3"], w3_scales, [nc.sync] * 4)
+        load_scale_rows(raw_scales["w3"], w3_scales)
         raw_words["w1"] = load_weight_words("w1_raw_words", w1_words)
         raw_words["w2"] = load_weight_words("w2_raw_words", w2_words)
         n4_list = load_list("n4_list", n4)
         offs_list = load_list("offs_list", offs)
         two_list = load_list("two_list", two)
-        load_scale_rows(raw_scales["w1"], w1_scales, [nc.sync] * 4)
-        load_scale_rows(raw_scales["w2"], w2_scales, [nc.sync] * 4)
+        load_scale_rows(raw_scales["w1"], w1_scales)
+        load_scale_rows(raw_scales["w2"], w2_scales)
         n1_list = load_list("n1_list", n1)
         n2_list = load_list("n2_list", n2)
         n3_list = load_list("n3_list", n3)
         n5_list = load_list("n5_list", n5)
         n6_list = load_list("n6_list", n6)
-        sl_col = load_column("sl_col", sl, nc.sync)
-        th_col = load_column("th_col", th, nc.sync)
-        sl2_col = load_column("sl2_col", sl2, nc.sync)
-        th2_col = load_column("th2_col", th2, nc.sync)
+        sl_col = load_by_slab("sl_col", sl)
+        th_col = load_by_slab("th_col", th)
+        sl2_col = load_by_slab("sl2_col", sl2)
+        th2_col = load_by_slab("th2_col", th2)
 
         dealt_words = {}
         dealt_scales = {}
         for name in ("w3", "w1", "w2"):
-            dealt_words[name] = sb(name + "_words", [P, 2 * N], U8)
-            dealt_scales[name] = sb(name + "_scales", [P, N], U8)
-            for dealt, raw, width in (
+            dealt_words[name] = sbuf(name + "_words", [P, 2 * N], U8)
+            dealt_scales[name] = sbuf(name + "_scales", [P, N], U8)
+            for dealt, raw, words_in_run in (
                 (dealt_words[name], raw_words[name], RUN // 2),
                 (dealt_scales[name], raw_scales[name], RUN // 4),
             ):
                 nc.scalar.copy(
-                    dealt[:].bitcast(U32).rearrange("p (t q e) -> p t q e", t=PACK, e=width),
-                    raw[:].bitcast(U32).rearrange("p (q t e) -> p t q e", t=PACK, e=width),
+                    dealt[:].bitcast(U32).rearrange("p (t q e) -> p t q e", t=PACK, e=words_in_run),
+                    raw[:].bitcast(U32).rearrange("p (q t e) -> p t q e", t=PACK, e=words_in_run),
                 )
 
         def first_layer(name, lst):
-            words = dealt_words[name]
-            scales = dealt_scales[name]
-            picked_words = sb(name + "_picked_words", [P, N], U32)
+            picked_words = sbuf(name + "_picked_words", [P, N], U32)
             nc.vector.tensor_copy(picked_words[:], x_word_table[:].bitcast(U32).indirect(lst[:]))
-            picked_scales = sb(name + "_picked_scales", [P, N], U8)
+            picked_scales = sbuf(name + "_picked_scales", [P, N], U8)
             nc.vector.tensor_copy(picked_scales[:], x_scale_table[:].indirect(lst[:]))
             banks = []
             for t in range(PACK):
                 bank = psum.tile([P, N], F32, name="bank")
                 nc.tensor.matmul_mx(
                     bank[:],
-                    lhsT=words[:, 2 * P * t : 2 * P * (t + 1)].bitcast(FP4X4),
-                    lhsT_scale=scales[:, P * t : P * (t + 1)],
+                    lhsT=dealt_words[name][:, 2 * P * t : 2 * P * (t + 1)].bitcast(FP4X4),
+                    lhsT_scale=dealt_scales[name][:, P * t : P * (t + 1)],
                     rhs=picked_words[:].bitcast(FP8X4),
                     rhs_scale=picked_scales[:],
                     start=True,
@@ -142,79 +143,93 @@ def tile_picked_twkclampbgclipecr_none_po_kernel(
                 banks.append(bank)
             return banks
 
-        def scaled_rows(name, bank, factor, on_scalar):
-            rows = sb(name, [P, N], F32)
+        def empty_bank(dst, bank, factor, on_scalar):
             if on_scalar:
-                nc.scalar.activation(rows[:], bank[:], ACT.Copy, scale=factor)
+                nc.scalar.activation(dst, bank[:], ACT.Copy, scale=factor)
             else:
-                nc.vector.tensor_scalar(rows[:], bank[:], factor, None, ALU.mult)
-            return rows
+                nc.vector.tensor_scalar(dst, bank[:], factor, None, ALU.mult)
 
-        def fetch(dst, rows, lst, lo, hi, on_vector):
-            if on_vector:
-                nc.vector.tensor_copy(dst, rows[:].indirect(cols(lst, lo, hi)))
+        def fetch(dst, plane, lst, lo, hi, on_scalar):
+            if on_scalar:
+                nc.scalar.activation(dst, plane[:].indirect(entries(lst, lo, hi)), ACT.Copy)
             else:
-                nc.scalar.activation(dst, rows[:].indirect(cols(lst, lo, hi)), ACT.Copy)
+                nc.vector.tensor_copy(dst, plane[:].indirect(entries(lst, lo, hi)))
 
         gain_bank = psum.tile([P, P], F32, name="bank")
         nc.tensor.transpose(gain_bank[:], gain_rows[:], identity[:])
-        gains = sb("gains", [P, 2 * PACK], F32)
+        gains = sbuf("gains", [P, 2 * PACK], F32)
         nc.scalar.copy(gains[:], gain_bank[:, : 2 * PACK])
         ga_col = gains[:, :PACK]
         gb_col = gains[:, PACK:]
 
         b_banks = first_layer("w3", three_list)
-        b_rows = [scaled_rows("b_rows%d" % t, b_banks[t], gb_col[:, t : t + 1], t == 0) for t in range(PACK)]
-        first_members = sb("first_members", [P, 1, PACK * N], BF16, "w1_raw_scales")
-        later_members = sb("later_members", [P, PACK - 1, PACK * N], BF16, "w2_raw_scales")
+        b_planes = []
+        for t in range(PACK):
+            plane = sbuf("b_plane%d" % t, [P, 2 * N], F32)
+            nc.vector.memset(plane[:, N:], 0.0)
+            b_planes.append(plane)
+        y_planes = [sbuf("y_plane%d" % t, [P, N], F32) for t in range(PACK)]
+        d_planes = [sbuf("d_plane%d" % t, [P, N], F32) for t in range(PACK)]
+        for t in range(PACK):
+            empty_bank(b_planes[t][:, :N], b_banks[t], gb_col[:, t : t + 1], t == 0)
+
+        first_members = sbuf("first_members", [P, 1, MEMBERS], BF16)
+        later_members = sbuf("later_members", [P, PACK - 1, MEMBERS], BF16, reuses="w2_raw_scales")
 
         def members(t_lo, t_hi):
             return first_members[:] if t_lo == 0 else later_members[:, t_lo - 1 : t_hi - 1, :]
 
         def fetch_members(t):
-            for lo in range(0, PACK * N, PIECE):
-                on_vector = t == PACK - 1 and lo >= PACK * N - MEMBER_PIECES_ON_VECTOR * PIECE
-                fetch(members(t, t + 1)[:, 0, lo : lo + PIECE], b_rows[t], n4_list, lo, lo + PIECE, on_vector)
+            split = MEMBERS - (MEMBERS_ON_VECTOR if t == PACK - 1 else 0)
+            for start, stop, on_scalar in ((0, split, True), (split, MEMBERS, False)):
+                for lo in range(start, stop, N):
+                    hi = min(lo + N, stop)
+                    fetch(members(t, t + 1)[:, 0, lo:hi], b_planes[t], n4_list, lo, hi, on_scalar)
 
-        z2_upper = sb("z2_upper", [P, PACK, N], BF16)
-        z2_lower = sb("z2_lower", [P, PACK, N], BF16)
+        z2_upper = sbuf("z2_upper", [P, PACK, N], BF16)
+        z2_lower = sbuf("z2_lower", [P, PACK, N], BF16)
 
-        def clamp_parts(t_lo, t_hi):
-            width = (t_hi - t_lo) * N
-            four = members(t_lo, t_hi).rearrange("p t (v u e) -> p (t v) u e", u=2, e=2)
-            hi = sb("hi%d" % t_lo, [P, width, 2], BF16, "w2_scales")
-            lo = sb("lo%d" % t_lo, [P, width, 2], BF16, "w2_words")
-            nc.vector.tensor_tensor(hi[:], four[:, :, 0, :], four[:, :, 1, :], ALU.max)
-            nc.vector.tensor_tensor(lo[:], four[:, :, 0, :], four[:, :, 1, :], ALU.min)
-            largest = sb("largest%d" % t_lo, [P, width], BF16)
-            nc.vector.tensor_tensor(largest[:], hi[:, :, 0], hi[:, :, 1], ALU.max)
+        def bounds(t_lo, t_hi):
+            columns = (t_hi - t_lo) * N
+            four = members(t_lo, t_hi).rearrange("p t (v g e) -> p (t v) g e", g=2, e=2)
+            pair_max = sbuf("pair_max%d" % t_lo, [P, columns, 2], BF16, reuses="w2_scales")
+            pair_min = sbuf("pair_min%d" % t_lo, [P, columns, 2], BF16, reuses="w2_words")
+            nc.vector.tensor_tensor(pair_max[:], four[:, :, 0, :], four[:, :, 1, :], ALU.max)
+            nc.vector.tensor_tensor(pair_min[:], four[:, :, 0, :], four[:, :, 1, :], ALU.min)
+            largest = sbuf("largest%d" % t_lo, [P, columns], BF16)
+            nc.vector.tensor_tensor(largest[:], pair_max[:, :, 0], pair_max[:, :, 1], ALU.max)
             nc.vector.tensor_tensor(
-                z2_lower[:, t_lo:t_hi, :].rearrange("p t v -> p (t v)"), lo[:, :, 0], lo[:, :, 1], ALU.min
+                z2_lower[:, t_lo:t_hi, :].rearrange("p t v -> p (t v)"), pair_min[:, :, 0], pair_min[:, :, 1], ALU.min
             )
             for t in range(t_lo, t_hi):
                 nc.vector.scalar_tensor_tensor(
-                    z2_upper[:, t, :], b_rows[t][:], 1.5, largest[:, N * (t - t_lo) : N * (t - t_lo + 1)], ALU.mult, ALU.min
+                    z2_upper[:, t, :], b_planes[t][:, :N], 1.5, largest[:, N * (t - t_lo) : N * (t - t_lo + 1)],
+                    ALU.mult, ALU.min,
                 )
 
         fetch_members(0)
-        ga_abs = sb("ga_abs", [P, PACK], F32)
-        ga_step = sb("ga_step", [P, PACK], F32)
-        ga_sign = sb("ga_sign", [P, PACK], F32)
+
+        ga_step = sbuf("ga_step", [P, PACK], F32)
+        ga_sign = sbuf("ga_sign", [P, PACK], F32)
+        ga_abs = sbuf("ga_abs", [P, PACK], F32)
+        ga_sign_bf = sbuf("ga_sign_bf", [P, PACK], BF16)
         nc.gpsimd.tensor_scalar(ga_step[:], ga_col, 0.0, 2.0, ALU.is_ge, ALU.mult)
         nc.gpsimd.tensor_scalar(ga_sign[:], ga_step[:], 1.0, -1.0, ALU.mult, ALU.add)
         nc.gpsimd.tensor_tensor(ga_abs[:], ga_col, ga_sign[:], ALU.mult)
-        ga_sign_bf = sb("ga_sign_bf", [P, PACK], BF16)
         nc.gpsimd.tensor_copy(ga_sign_bf[:], ga_sign[:])
+
         y_banks = first_layer("w1", offs_list)
-        y_rows = [scaled_rows("y_rows%d" % t, y_banks[t], ga_abs[:, t : t + 1], False) for t in range(PACK)]
+        for t in range(PACK):
+            empty_bank(y_planes[t][:], y_banks[t], ga_abs[:, t : t + 1], False)
         fetch_members(1)
         d_banks = first_layer("w2", two_list)
-        d_rows = [scaled_rows("d_rows%d" % t, d_banks[t], ga_abs[:, t : t + 1], False) for t in range(PACK)]
+        for t in range(PACK):
+            empty_bank(d_planes[t][:], d_banks[t], ga_abs[:, t : t + 1], False)
 
-        neg_th = sb("neg_th", [P, PACK], F32)
-        bias1 = sb("bias1", [P, PACK], F32)
-        scale2 = sb("scale2", [P, PACK], F32)
-        bias2 = sb("bias2", [P, PACK], F32)
+        neg_th = sbuf("neg_th", [P, PACK], F32)
+        bias1 = sbuf("bias1", [P, PACK], F32)
+        scale2 = sbuf("scale2", [P, PACK], F32)
+        bias2 = sbuf("bias2", [P, PACK], F32)
         nc.gpsimd.tensor_scalar(neg_th[:], th_col[:], -1.0, 0.0, ALU.mult, ALU.add)
         nc.gpsimd.tensor_tensor(bias1[:], sl_col[:], neg_th[:], ALU.mult)
         nc.gpsimd.tensor_scalar(scale2[:], sl2_col[:], -1.0, 0.0, ALU.mult, ALU.add)
@@ -222,123 +237,125 @@ def tile_picked_twkclampbgclipecr_none_po_kernel(
 
         fetch_members(2)
         fetch_members(3)
-        clamp_parts(0, 1)
-        clamp_parts(1, 3)
-        clamp_parts(3, 4)
+        bounds(0, 1)
+        bounds(1, 3)
+        bounds(3, 4)
 
-        z2_planes = sb("z2_planes", [P, PACK, N], BF16)
+        z2_planes = sbuf("z2_planes", [P, PACK, N], BF16)
         nc.vector.tensor_tensor(z2_planes[:], z2_upper[:], z2_lower[:], ALU.max)
-        z2_bf = sb("z2_bf", [P, N, PACK], BF16)
+        z2_woven = sbuf("z2_woven", [P, N, PACK], BF16)
         nc.vector.tensor_copy(
-            z2_bf[:].rearrange("p (c i) t -> p c t i", i=4), z2_planes[:].rearrange("p t (c i) -> p c t i", i=4)
+            z2_woven[:].rearrange("p (c i) t -> p c t i", i=4), z2_planes[:].rearrange("p t (c i) -> p c t i", i=4)
         )
-        z2_codes = sb("z2_codes", [P, N], U32)
-        z2_scales = sb("z2_scales", [P, N], U8)
-        nc.vector.quantize_mx(z2_codes[:].bitcast(FP8X4), z2_scales[:], z2_bf[:].rearrange("p v t -> p (v t)"))
+        z2_codes = sbuf("z2_codes", [P, N], U32)
+        z2_scales = sbuf("z2_scales", [P, N], U8)
+        nc.vector.quantize_mx(z2_codes[:].bitcast(FP8X4), z2_scales[:], z2_woven[:].rearrange("p v t -> p (v t)"))
 
-        y_at_n1 = sb("y_at_n1", [P, PACK, N], F32)
-        d_at_n2 = sb("d_at_n2", [P, PACK, N], BF16)
-        d_at_n3 = sb("d_at_n3", [P, PACK, N], BF16)
-        y_less = sb("y_less", [P, PACK, N], BF16)
-        capped = sb("capped", [P, PACK, N], BF16)
-        held = sb("held", [P, PACK, N], BF16)
-        z_bf = sb("z_bf", [P, PACK, P, PACK], BF16)
+        y_at_n1 = sbuf("y_at_n1", [P, PACK, N], F32)
+        d_at_n2 = sbuf("d_at_n2", [P, PACK, N], BF16)
+        d_at_n3 = sbuf("d_at_n3", [P, PACK, N], BF16)
+        y_less = sbuf("y_less", [P, PACK, N], BF16)
+        capped = sbuf("capped", [P, PACK, N], BF16)
+        held = sbuf("held", [P, PACK, N], BF16)
+        z_woven = sbuf("z_woven", [P, PACK, P, PACK], BF16)
+        held_woven = sbuf("held_woven", [P, PACK, P, PACK], BF16)
 
-        unsigned = sb("unsigned", [P, PACK, P, PACK], BF16)
-
-        def deal(lo, hi):
+        def weave(lo, hi):
             nc.vector.tensor_copy(
-                unsigned[:, :, lo // PACK : hi // PACK, :].rearrange("p u (c i) t -> p c u i t", i=2),
+                held_woven[:, :, lo // PACK : hi // PACK, :].rearrange("p u (c i) t -> p c u i t", i=2),
                 held[:, :, lo:hi].rearrange("p t (c i u) -> p c u i t", i=2, u=PACK),
             )
 
         def give_sign(lo, hi, u_lo, u_hi):
-            at = slice(lo // PACK, hi // PACK)
+            m_range = slice(lo // PACK, hi // PACK)
             signs = ga_sign_bf[:].unsqueeze(1).unsqueeze(1).to_broadcast([P, u_hi - u_lo, (hi - lo) // PACK, PACK])
-            nc.vector.tensor_tensor(z_bf[:, u_lo:u_hi, at, :], unsigned[:, u_lo:u_hi, at, :], signs, ALU.mult)
+            nc.vector.tensor_tensor(z_woven[:, u_lo:u_hi, m_range, :], held_woven[:, u_lo:u_hi, m_range, :], signs, ALU.mult)
 
         for t in range(PACK):
-            for lo in range(0, N, PIECE):
-                fetch(y_at_n1[:, t, lo : lo + PIECE], y_rows[t], n1_list, lo, lo + PIECE, False)
-            nc.vector.scalar_tensor_tensor(y_less[:, t, :], y_at_n1[:, t, :], -0.5, y_rows[t][:], ALU.mult, ALU.add)
-        for lo in range(0, N, PIECE):
+            for lo in range(0, N, HALF):
+                fetch(y_at_n1[:, t, lo : lo + HALF], y_planes[t], n1_list, lo, lo + HALF, True)
+            nc.vector.scalar_tensor_tensor(y_less[:, t, :], y_at_n1[:, t, :], -0.5, y_planes[t][:], ALU.mult, ALU.add)
+        for lo in range(0, N, HALF):
+            half = slice(lo, lo + HALF)
             for t in range(PACK):
-                fetch(d_at_n2[:, t, lo : lo + PIECE], d_rows[t], n2_list, lo, lo + PIECE, False)
-            at = slice(lo, lo + PIECE)
-            nc.vector.tensor_tensor(capped[:, :, at], y_less[:, :, at], d_at_n2[:, :, at], ALU.min)
-        for lo, hi in Z_PIECES:
+                fetch(d_at_n2[:, t, half], d_planes[t], n2_list, lo, lo + HALF, True)
+            nc.vector.tensor_tensor(capped[:, :, half], y_less[:, :, half], d_at_n2[:, :, half], ALU.min)
+        for lo, hi in PIECES:
             for t in range(PACK):
-                fetch(d_at_n3[:, t, lo:hi], d_rows[t], n3_list, lo, hi, False)
+                fetch(d_at_n3[:, t, lo:hi], d_planes[t], n3_list, lo, hi, True)
             nc.vector.tensor_tensor(held[:, :, lo:hi], capped[:, :, lo:hi], d_at_n3[:, :, lo:hi], ALU.max)
-            deal(lo, hi)
+            weave(lo, hi)
             if hi < N:
                 give_sign(lo, hi, 0, PACK)
 
-        z_codes = sb("z_codes", [P, N], U32)
-        z_scales = sb("z_scales", [P, N], U8)
-        s_rows = []
+        last_lo = PIECES[-1][0]
+        z_codes = sbuf("z_codes", [P, N], U32)
+        z_scales = sbuf("z_scales", [P, N], U8)
+        s_slabs = []
         for u in range(PACK):
-            if u < 2:
-                give_sign(Z_PIECES[-1][0], N, u, 1 if u == 0 else PACK)
-            at = slice(P * u, P * (u + 1))
-            nc.vector.quantize_mx(z_codes[:, at].bitcast(FP8X4), z_scales[:, at], z_bf[:, u].rearrange("p m t -> p (m t)"))
-            rows = sb("s_rows%d" % u, [P, N], F32)
-            width = N // 2 if u == 0 else N
-            for lo in range(0, N, width):
-                part = slice(lo, lo + width)
-                bank = psum.tile([P, width], F32, name="bank")
+            if u == 0:
+                give_sign(last_lo, N, 0, 1)
+            if u == 1:
+                give_sign(last_lo, N, 1, PACK)
+            stationary = slice(P * u, P * (u + 1))
+            nc.vector.quantize_mx(
+                z_codes[:, stationary].bitcast(FP8X4), z_scales[:, stationary], z_woven[:, u].rearrange("p m t -> p (m t)")
+            )
+            slab = sbuf("s_slab%d" % u, [P, N], F32)
+            bank_columns = HALF if u == 0 else N
+            for lo in range(0, N, bank_columns):
+                moving = slice(lo, lo + bank_columns)
+                bank = psum.tile([P, bank_columns], F32, name="bank")
                 nc.tensor.matmul_mx(
                     bank[:],
-                    lhsT=z_codes[:, at].bitcast(FP8X4),
-                    lhsT_scale=z_scales[:, at],
-                    rhs=z2_codes[:, part].bitcast(FP8X4),
-                    rhs_scale=z2_scales[:, part],
+                    lhsT=z_codes[:, stationary].bitcast(FP8X4),
+                    lhsT_scale=z_scales[:, stationary],
+                    rhs=z2_codes[:, moving].bitcast(FP8X4),
+                    rhs_scale=z2_scales[:, moving],
                     start=True,
                     stop=True,
                 )
-                if lo > 0:
-                    nc.scalar.activation(rows[:, part], bank[:], ACT.Copy, scale=0.0625)
-                else:
-                    nc.vector.tensor_scalar(rows[:, part], bank[:], 0.0625, None, ALU.mult)
-            s_rows.append(rows)
+                empty_bank(slab[:, moving], bank, 0.0625, lo > 0)
+            s_slabs.append(slab)
 
-        gate1 = sb("gate1", [P, PACK, N], F32)
-        gate2 = sb("gate2", [P, PACK, N], F32)
-        half_gated = sb("half_gated", [P, PACK, N], F32)
-        result = sb("result", [P, PACK, N], F32)
-        result_bf = sb("result_bf", [P, N, PACK], BF16)
-        result_codes = sb("result_codes", [P, N], I32)
-        result_scales = sb("result_scales", [P, N], U8)
+        gate1 = sbuf("gate1", [P, PACK, N], F32)
+        gate2 = sbuf("gate2", [P, PACK, N], F32)
+        once_gated = sbuf("once_gated", [P, PACK, N], F32)
+        result = sbuf("result", [P, PACK, N], F32)
+        result_woven = sbuf("result_woven", [P, N, PACK], BF16)
+        result_codes = sbuf("result_codes", [P, N], I32)
+        result_scales = sbuf("result_scales", [P, N], U8)
         out_rows = out_0.rearrange("(p u) v -> p u v", u=PACK)
         out_words = out_1[0].rearrange("p v r -> p (v r)").bitcast(I32)
-        for lo, hi in OUT_PIECES:
-            if lo % PIECE == 0:
-                at = slice(lo, lo + PIECE)
-                for u in range(PACK):
-                    nc.scalar.activation(
-                        gate1[:, u, at], s_rows[u][:].indirect(cols(n5_list, lo, lo + PIECE)), ACT.Sigmoid,
-                        bias=bias1[:, u : u + 1], scale=sl_col[:, u : u + 1],
-                    )
-                    nc.vector.scalar_tensor_tensor(half_gated[:, u, at], s_rows[u][:, at], 2.0, gate1[:, u, at], ALU.mult, ALU.mult)
+        for lo, hi in PIECES:
             for u in range(PACK):
                 nc.scalar.activation(
-                    gate2[:, u, lo:hi], s_rows[u][:].indirect(cols(n6_list, lo, hi)), ACT.Sigmoid,
+                    gate1[:, u, lo:hi], s_slabs[u][:].indirect(entries(n5_list, lo, hi)), ACT.Sigmoid,
+                    bias=bias1[:, u : u + 1], scale=sl_col[:, u : u + 1],
+                )
+                nc.scalar.activation(
+                    gate2[:, u, lo:hi], s_slabs[u][:].indirect(entries(n6_list, lo, hi)), ACT.Sigmoid,
                     bias=bias2[:, u : u + 1], scale=scale2[:, u : u + 1],
+                )
+                nc.vector.scalar_tensor_tensor(
+                    once_gated[:, u, lo:hi], s_slabs[u][:, lo:hi], 2.0, gate1[:, u, lo:hi], ALU.mult, ALU.mult
                 )
             for u_lo, u_hi in ((0, PACK - 1), (PACK - 1, PACK)) if hi == N else ((0, PACK),):
                 nc.vector.tensor_tensor(
-                    result[:, u_lo:u_hi, lo:hi], half_gated[:, u_lo:u_hi, lo:hi], gate2[:, u_lo:u_hi, lo:hi], ALU.mult
+                    result[:, u_lo:u_hi, lo:hi], once_gated[:, u_lo:u_hi, lo:hi], gate2[:, u_lo:u_hi, lo:hi], ALU.mult
                 )
             nc.sync.dma_start(out_rows[:, :, lo:hi], result[:, :, lo:hi])
             nc.vector.tensor_copy(
-                result_bf[:, lo:hi, :].rearrange("p (c i) u -> p c u i", i=4),
+                result_woven[:, lo:hi, :].rearrange("p (c i) u -> p c u i", i=4),
                 result[:, :, lo:hi].rearrange("p u (c i) -> p c u i", i=4),
             )
             nc.vector.quantize_mx(
                 result_codes[:, lo:hi].bitcast(FP8X4), result_scales[:, lo:hi],
-                result_bf[:, lo:hi, :].rearrange("p v u -> p (v u)"),
+                result_woven[:, lo:hi, :].rearrange("p v u -> p (v u)"),
             )
             nc.sync.dma_start(out_words[:, lo:hi], result_codes[:, lo:hi])
-        for q in range(4):
-            queue = nc.scalar if q % 2 == 0 else nc.sync
-            queue.dma_start(out_2[0, 4 * q : 4 * q + 4, :].bitcast(I32), result_scales[32 * q : 32 * q + 4, :].bitcast(I32))
+        for quad in range(QUADRANTS):
+            queue = nc.scalar if quad % 2 == 0 else nc.sync
+            queue.dma_start(
+                out_2[0, 4 * quad : 4 * quad + 4, :].bitcast(I32), result_scales[32 * quad : 32 * quad + 4, :].bitcast(I32)
+            )

from contextlib import ExitStack

import concourse.mybir as mybir
from concourse.masks import make_identity

FLOPS = 4 * 2 * 512 * 512 * 512

F32 = mybir.dt.float32
BF16 = mybir.dt.bfloat16
I32 = mybir.dt.int32
U32 = mybir.dt.uint32
U16 = mybir.dt.uint16
U8 = mybir.dt.uint8
FP8X4 = mybir.dt.float8_e4m3fn_x4
FP4X4 = mybir.dt.float4_e2m1fn_x4
ALU = mybir.AluOpType
ACT = mybir.ActivationFunctionType

P = 128
PACK = 4
QUADRANTS = 4
N = 512
TOKENS = 2048
MEMBERS = 4 * N
RUN = 8
HALF = N // 2
PIECES = ((0, 256), (256, 384), (384, 512))
MEMBERS_ON_VECTOR = 1152


def tile_picked_twkclampbgclipecr_none_po_kernel(
    tc, x_words, x_scales, w1_words, w1_scales, w2_words, w2_scales, w3_words, w3_scales,
    ga, gb, sl, th, sl2, th2, offs, two, n1, n2, n3, three, n4, n5, n6, out_0, out_1, out_2,
):
    nc = tc.nc
    with ExitStack() as ctx:
        keep = ctx.enter_context(tc.tile_pool(name="keep", bufs=1))
        psum = ctx.enter_context(tc.psum_pool(name="psum", bufs=8))

        def sbuf(name, shape, dtype, reuses=None):
            return keep.tile(shape, dtype, name=name, tag=reuses or name, align_bytes=64)

        def load_list(name, src):
            lst = keep.tile(list(src.shape), U16, name=name)
            nc.sync.dma_start(lst[:], src)
            return lst

        def load_by_slab(name, src):
            col = sbuf(name, [P, PACK], F32)
            nc.sync.dma_start(col[:], src.rearrange("(p u) o -> p (u o)", u=PACK))
            return col

        def load_scale_rows(dst, src):
            for quad in range(QUADRANTS):
                nc.sync.dma_start(
                    dst[32 * quad : 32 * quad + 4, :].bitcast(I32), src[0, 4 * quad : 4 * quad + 4, :].bitcast(I32)
                )

        def load_weight_words(name, src):
            raw = sbuf(name, [P, 2 * N], U8)
            nc.sync.dma_start(raw[:].bitcast(I32), src[0].bitcast(I32))
            return raw

        def entries(lst, lo, hi):
            return lst[:, lo // 16 : hi // 16]

        warm_in = sbuf("warm_in", [P, 1], F32)
        warm_out = sbuf("warm_out", [P, 1], F32)
        nc.vector.memset(warm_in[:], 0.0)
        nc.scalar.activation(warm_out[:], warm_in[:], ACT.Sigmoid)

        x_scale_table = sbuf("x_scale_table", [P, TOKENS], U8)
        nc.vector.memset(x_scale_table[:].bitcast(I32), 0)
        raw_scales = {}
        for name in ("w3", "w1", "w2"):
            raw_scales[name] = sbuf(name + "_raw_scales", [P, N], U8)
            nc.vector.memset(raw_scales[name][:].bitcast(I32), 0)

        gain_rows = sbuf("gain_rows", [P, P], F32)
        nc.gpsimd.memset(gain_rows[:], 0.0)
        for row, src in ((PACK, gb), (0, ga)):
            nc.gpsimd.dma_start(
                gain_rows[row : row + PACK, :].rearrange("t (q e) -> t q e", e=RUN),
                src.rearrange("(q t e) o -> t q (e o)", t=PACK, e=RUN),
            )
        identity = sbuf("identity", [P, P], F32)
        make_identity(nc, identity[:])

        x_word_table = sbuf("x_word_table", [P, TOKENS], I32)
        nc.sync.dma_start(x_word_table[:], x_words[0].rearrange("p n r -> p (n r)").bitcast(I32))
        three_list = load_list("three_list", three)
        load_scale_rows(x_scale_table, x_scales)
        raw_words = {"w3": load_weight_words("w3_raw_words", w3_words)}
        load_scale_rows(raw_scales["w3"], w3_scales)
        raw_words["w1"] = load_weight_words("w1_raw_words", w1_words)
        raw_words["w2"] = load_weight_words("w2_raw_words", w2_words)
        n4_list = load_list("n4_list", n4)
        offs_list = load_list("offs_list", offs)
        two_list = load_list("two_list", two)
        load_scale_rows(raw_scales["w1"], w1_scales)
        load_scale_rows(raw_scales["w2"], w2_scales)
        n1_list = load_list("n1_list", n1)
        n2_list = load_list("n2_list", n2)
        n3_list = load_list("n3_list", n3)
        n5_list = load_list("n5_list", n5)
        n6_list = load_list("n6_list", n6)
        sl_col = load_by_slab("sl_col", sl)
        th_col = load_by_slab("th_col", th)
        sl2_col = load_by_slab("sl2_col", sl2)
        th2_col = load_by_slab("th2_col", th2)

        dealt_words = {}
        dealt_scales = {}
        for name in ("w3", "w1", "w2"):
            dealt_words[name] = sbuf(name + "_words", [P, 2 * N], U8)
            dealt_scales[name] = sbuf(name + "_scales", [P, N], U8)
            for dealt, raw, words_in_run in (
                (dealt_words[name], raw_words[name], RUN // 2),
                (dealt_scales[name], raw_scales[name], RUN // 4),
            ):
                nc.scalar.copy(
                    dealt[:].bitcast(U32).rearrange("p (t q e) -> p t q e", t=PACK, e=words_in_run),
                    raw[:].bitcast(U32).rearrange("p (q t e) -> p t q e", t=PACK, e=words_in_run),
                )

        def first_layer(name, lst):
            picked_words = sbuf(name + "_picked_words", [P, N], U32)
            nc.vector.tensor_copy(picked_words[:], x_word_table[:].bitcast(U32).indirect(lst[:]))
            picked_scales = sbuf(name + "_picked_scales", [P, N], U8)
            nc.vector.tensor_copy(picked_scales[:], x_scale_table[:].indirect(lst[:]))
            banks = []
            for t in range(PACK):
                bank = psum.tile([P, N], F32, name="bank")
                nc.tensor.matmul_mx(
                    bank[:],
                    lhsT=dealt_words[name][:, 2 * P * t : 2 * P * (t + 1)].bitcast(FP4X4),
                    lhsT_scale=dealt_scales[name][:, P * t : P * (t + 1)],
                    rhs=picked_words[:].bitcast(FP8X4),
                    rhs_scale=picked_scales[:],
                    start=True,
                    stop=True,
                )
                banks.append(bank)
            return banks

        def empty_bank(dst, bank, factor, on_scalar):
            if on_scalar:
                nc.scalar.activation(dst, bank[:], ACT.Copy, scale=factor)
            else:
                nc.vector.tensor_scalar(dst, bank[:], factor, None, ALU.mult)

        def fetch(dst, plane, lst, lo, hi, on_scalar):
            if on_scalar:
                nc.scalar.activation(dst, plane[:].indirect(entries(lst, lo, hi)), ACT.Copy)
            else:
                nc.vector.tensor_copy(dst, plane[:].indirect(entries(lst, lo, hi)))

        gain_bank = psum.tile([P, P], F32, name="bank")
        nc.tensor.transpose(gain_bank[:], gain_rows[:], identity[:])
        gains = sbuf("gains", [P, 2 * PACK], F32)
        nc.scalar.copy(gains[:], gain_bank[:, : 2 * PACK])
        ga_col = gains[:, :PACK]
        gb_col = gains[:, PACK:]

        b_banks = first_layer("w3", three_list)
        b_planes = []
        for t in range(PACK):
            plane = sbuf("b_plane%d" % t, [P, 2 * N], F32)
            nc.vector.memset(plane[:, N:], 0.0)
            b_planes.append(plane)
        y_planes = [sbuf("y_plane%d" % t, [P, N], F32) for t in range(PACK)]
        d_planes = [sbuf("d_plane%d" % t, [P, N], F32) for t in range(PACK)]
        for t in range(PACK):
            empty_bank(b_planes[t][:, :N], b_banks[t], gb_col[:, t : t + 1], t == 0)

        first_members = sbuf("first_members", [P, 1, MEMBERS], BF16)
        later_members = sbuf("later_members", [P, PACK - 1, MEMBERS], BF16, reuses="w2_raw_scales")

        def members(t_lo, t_hi):
            return first_members[:] if t_lo == 0 else later_members[:, t_lo - 1 : t_hi - 1, :]

        def fetch_members(t):
            split = MEMBERS - (MEMBERS_ON_VECTOR if t == PACK - 1 else 0)
            for start, stop, on_scalar in ((0, split, True), (split, MEMBERS, False)):
                for lo in range(start, stop, N):
                    hi = min(lo + N, stop)
                    fetch(members(t, t + 1)[:, 0, lo:hi], b_planes[t], n4_list, lo, hi, on_scalar)

        z2_upper = sbuf("z2_upper", [P, PACK, N], BF16)
        z2_lower = sbuf("z2_lower", [P, PACK, N], BF16)

        def bounds(t_lo, t_hi):
            columns = (t_hi - t_lo) * N
            four = members(t_lo, t_hi).rearrange("p t (v g e) -> p (t v) g e", g=2, e=2)
            pair_max = sbuf("pair_max%d" % t_lo, [P, columns, 2], BF16, reuses="w2_scales")
            pair_min = sbuf("pair_min%d" % t_lo, [P, columns, 2], BF16, reuses="w2_words")
            nc.vector.tensor_tensor(pair_max[:], four[:, :, 0, :], four[:, :, 1, :], ALU.max)
            nc.vector.tensor_tensor(pair_min[:], four[:, :, 0, :], four[:, :, 1, :], ALU.min)
            largest = sbuf("largest%d" % t_lo, [P, columns], BF16)
            nc.vector.tensor_tensor(largest[:], pair_max[:, :, 0], pair_max[:, :, 1], ALU.max)
            nc.vector.tensor_tensor(
                z2_lower[:, t_lo:t_hi, :].rearrange("p t v -> p (t v)"), pair_min[:, :, 0], pair_min[:, :, 1], ALU.min
            )
            for t in range(t_lo, t_hi):
                nc.vector.scalar_tensor_tensor(
                    z2_upper[:, t, :], b_planes[t][:, :N], 1.5, largest[:, N * (t - t_lo) : N * (t - t_lo + 1)],
                    ALU.mult, ALU.min,
                )

        fetch_members(0)

        ga_step = sbuf("ga_step", [P, PACK], F32)
        ga_sign = sbuf("ga_sign", [P, PACK], F32)
        ga_abs = sbuf("ga_abs", [P, PACK], F32)
        ga_sign_bf = sbuf("ga_sign_bf", [P, PACK], BF16)
        nc.gpsimd.tensor_scalar(ga_step[:], ga_col, 0.0, 2.0, ALU.is_ge, ALU.mult)
        nc.gpsimd.tensor_scalar(ga_sign[:], ga_step[:], 1.0, -1.0, ALU.mult, ALU.add)
        nc.gpsimd.tensor_tensor(ga_abs[:], ga_col, ga_sign[:], ALU.mult)
        nc.gpsimd.tensor_copy(ga_sign_bf[:], ga_sign[:])

        y_banks = first_layer("w1", offs_list)
        for t in range(PACK):
            empty_bank(y_planes[t][:], y_banks[t], ga_abs[:, t : t + 1], False)
        fetch_members(1)
        d_banks = first_layer("w2", two_list)
        for t in range(PACK):
            empty_bank(d_planes[t][:], d_banks[t], ga_abs[:, t : t + 1], False)

        neg_th = sbuf("neg_th", [P, PACK], F32)
        bias1 = sbuf("bias1", [P, PACK], F32)
        scale2 = sbuf("scale2", [P, PACK], F32)
        bias2 = sbuf("bias2", [P, PACK], F32)
        nc.gpsimd.tensor_scalar(neg_th[:], th_col[:], -1.0, 0.0, ALU.mult, ALU.add)
        nc.gpsimd.tensor_tensor(bias1[:], sl_col[:], neg_th[:], ALU.mult)
        nc.gpsimd.tensor_scalar(scale2[:], sl2_col[:], -1.0, 0.0, ALU.mult, ALU.add)
        nc.gpsimd.tensor_tensor(bias2[:], sl2_col[:], th2_col[:], ALU.mult)

        fetch_members(2)
        fetch_members(3)
        bounds(0, 1)
        bounds(1, 3)
        bounds(3, 4)

        z2_planes = sbuf("z2_planes", [P, PACK, N], BF16)
        nc.vector.tensor_tensor(z2_planes[:], z2_upper[:], z2_lower[:], ALU.max)
        z2_woven = sbuf("z2_woven", [P, N, PACK], BF16)
        nc.vector.tensor_copy(
            z2_woven[:].rearrange("p (c i) t -> p c t i", i=4), z2_planes[:].rearrange("p t (c i) -> p c t i", i=4)
        )
        z2_codes = sbuf("z2_codes", [P, N], U32)
        z2_scales = sbuf("z2_scales", [P, N], U8)
        nc.vector.quantize_mx(z2_codes[:].bitcast(FP8X4), z2_scales[:], z2_woven[:].rearrange("p v t -> p (v t)"))

        y_at_n1 = sbuf("y_at_n1", [P, PACK, N], F32)
        d_at_n2 = sbuf("d_at_n2", [P, PACK, N], BF16)
        d_at_n3 = sbuf("d_at_n3", [P, PACK, N], BF16)
        y_less = sbuf("y_less", [P, PACK, N], BF16)
        capped = sbuf("capped", [P, PACK, N], BF16)
        held = sbuf("held", [P, PACK, N], BF16)
        z_woven = sbuf("z_woven", [P, PACK, P, PACK], BF16)
        held_woven = sbuf("held_woven", [P, PACK, P, PACK], BF16)

        def weave(lo, hi):
            nc.vector.tensor_copy(
                held_woven[:, :, lo // PACK : hi // PACK, :].rearrange("p u (c i) t -> p c u i t", i=2),
                held[:, :, lo:hi].rearrange("p t (c i u) -> p c u i t", i=2, u=PACK),
            )

        def give_sign(lo, hi, u_lo, u_hi):
            m_range = slice(lo // PACK, hi // PACK)
            signs = ga_sign_bf[:].unsqueeze(1).unsqueeze(1).to_broadcast([P, u_hi - u_lo, (hi - lo) // PACK, PACK])
            nc.vector.tensor_tensor(z_woven[:, u_lo:u_hi, m_range, :], held_woven[:, u_lo:u_hi, m_range, :], signs, ALU.mult)

        for t in range(PACK):
            for lo in range(0, N, HALF):
                fetch(y_at_n1[:, t, lo : lo + HALF], y_planes[t], n1_list, lo, lo + HALF, True)
            nc.vector.scalar_tensor_tensor(y_less[:, t, :], y_at_n1[:, t, :], -0.5, y_planes[t][:], ALU.mult, ALU.add)
        for lo in range(0, N, HALF):
            half = slice(lo, lo + HALF)
            for t in range(PACK):
                fetch(d_at_n2[:, t, half], d_planes[t], n2_list, lo, lo + HALF, True)
            nc.vector.tensor_tensor(capped[:, :, half], y_less[:, :, half], d_at_n2[:, :, half], ALU.min)
        for lo, hi in PIECES:
            for t in range(PACK):
                fetch(d_at_n3[:, t, lo:hi], d_planes[t], n3_list, lo, hi, True)
            nc.vector.tensor_tensor(held[:, :, lo:hi], capped[:, :, lo:hi], d_at_n3[:, :, lo:hi], ALU.max)
            weave(lo, hi)
            if hi < N:
                give_sign(lo, hi, 0, PACK)

        last_lo = PIECES[-1][0]
        z_codes = sbuf("z_codes", [P, N], U32)
        z_scales = sbuf("z_scales", [P, N], U8)
        s_slabs = []
        for u in range(PACK):
            if u == 0:
                give_sign(last_lo, N, 0, 1)
            if u == 1:
                give_sign(last_lo, N, 1, PACK)
            stationary = slice(P * u, P * (u + 1))
            nc.vector.quantize_mx(
                z_codes[:, stationary].bitcast(FP8X4), z_scales[:, stationary], z_woven[:, u].rearrange("p m t -> p (m t)")
            )
            slab = sbuf("s_slab%d" % u, [P, N], F32)
            bank_columns = HALF if u == 0 else N
            for lo in range(0, N, bank_columns):
                moving = slice(lo, lo + bank_columns)
                bank = psum.tile([P, bank_columns], F32, name="bank")
                nc.tensor.matmul_mx(
                    bank[:],
                    lhsT=z_codes[:, stationary].bitcast(FP8X4),
                    lhsT_scale=z_scales[:, stationary],
                    rhs=z2_codes[:, moving].bitcast(FP8X4),
                    rhs_scale=z2_scales[:, moving],
                    start=True,
                    stop=True,
                )
                empty_bank(slab[:, moving], bank, 0.0625, lo > 0)
            s_slabs.append(slab)

        gate1 = sbuf("gate1", [P, PACK, N], F32)
        gate2 = sbuf("gate2", [P, PACK, N], F32)
        once_gated = sbuf("once_gated", [P, PACK, N], F32)
        result = sbuf("result", [P, PACK, N], F32)
        result_woven = sbuf("result_woven", [P, N, PACK], BF16)
        result_codes = sbuf("result_codes", [P, N], I32)
        result_scales = sbuf("result_scales", [P, N], U8)
        out_rows = out_0.rearrange("(p u) v -> p u v", u=PACK)
        out_words = out_1[0].rearrange("p v r -> p (v r)").bitcast(I32)
        for lo, hi in PIECES:
            for u in range(PACK):
                nc.scalar.activation(
                    gate1[:, u, lo:hi], s_slabs[u][:].indirect(entries(n5_list, lo, hi)), ACT.Sigmoid,
                    bias=bias1[:, u : u + 1], scale=sl_col[:, u : u + 1],
                )
                nc.scalar.activation(
                    gate2[:, u, lo:hi], s_slabs[u][:].indirect(entries(n6_list, lo, hi)), ACT.Sigmoid,
                    bias=bias2[:, u : u + 1], scale=scale2[:, u : u + 1],
                )
                nc.vector.scalar_tensor_tensor(
                    once_gated[:, u, lo:hi], s_slabs[u][:, lo:hi], 2.0, gate1[:, u, lo:hi], ALU.mult, ALU.mult
                )
            for u_lo, u_hi in ((0, PACK - 1), (PACK - 1, PACK)) if hi == N else ((0, PACK),):
                nc.vector.tensor_tensor(
                    result[:, u_lo:u_hi, lo:hi], once_gated[:, u_lo:u_hi, lo:hi], gate2[:, u_lo:u_hi, lo:hi], ALU.mult
                )
            nc.sync.dma_start(out_rows[:, :, lo:hi], result[:, :, lo:hi])
            nc.vector.tensor_copy(
                result_woven[:, lo:hi, :].rearrange("p (c i) u -> p c u i", i=4),
                result[:, :, lo:hi].rearrange("p u (c i) -> p c u i", i=4),
            )
            nc.vector.quantize_mx(
                result_codes[:, lo:hi].bitcast(FP8X4), result_scales[:, lo:hi],
                result_woven[:, lo:hi, :].rearrange("p v u -> p (v u)"),
            )
            nc.sync.dma_start(out_words[:, lo:hi], result_codes[:, lo:hi])
        for quad in range(QUADRANTS):
            queue = nc.scalar if quad % 2 == 0 else nc.sync
            queue.dma_start(
                out_2[0, 4 * quad : 4 * quad + 4, :].bitcast(I32), result_scales[32 * quad : 32 * quad + 4, :].bitcast(I32)
            )
